import numpy as np
CORES = [1,2,9,10,17,18,25,26,33,34,41,42,49,50,57,58,65,66,73,74,81,82,89,90,97,98,105,106,113,114,121,122]
N = 32
T = 512
ROUTE = [[[9],[25],[27],[12],[30],[9],[9],[21],[9],[9],[9],[23],[24],[9],[2],[9],[9],[9],[0],[9],[31],[9],[6],[9],[19],[22],[9],[24],[13],[6],[17],[18],[7],[9],[17],[9],[9],[9],[31],[22],[19],[31],[9],[4],[9],[12],[25],[9],[10],[9],[9],[29],[9],[25],[21],[9],[1],[9],[22],[9],[9],[19],[11],[28],[9],[6],[9],[9],[13],[21],[5],[0],[22],[9],[24],[9],[29],[9],[5],[16],[9],[9],[11],[24],[12],[3],[1],[0],[25],[28],[9],[29],[20],[24],[5],[25],[13],[9],[13],[18],[28],[9],[12],[3],[27],[7],[9],[9],[15],[19],[6],[3],[12],[9],[25],[21],[19],[28],[24],[6],[9],[27],[9],[26],[10],[31],[18],[9],[9],[30],[18],[13],[31],[9],[26],[15],[9],[18],[14],[11],[9],[14],[13],[9],[9],[11],[8],[9],[9],[9],[7],[23],[2],[28],[9],[17],[19],[11],[30],[27],[31],[19],[21],[9],[26],[9],[2],[14],[22],[9],[9],[19],[9],[23],[6],[14],[9],[9],[9],[5],[26],[9],[15],[3],[21],[16],[17],[2],[9],[11],[9],[20],[9],[8],[12],[9],[9],[9],[9],[29],[27],[15],[31],[9],[20],[9],[9],[3],[15],[9],[9],[23],[9],[0],[30],[9],[12],[21],[9],[9],[6],[20],[5],[29],[11],[9],[25],[9],[9],[9],[9],[9],[28],[11],[9],[9],[9],[23],[9],[9],[29],[29],[24],[21],[9],[9],[9],[0],[11],[5],[29],[9],[12],[27],[18],[9],[4],[9],[9],[30],[16],[26],[9],[9],[13],[9],[19],[9],[30],[20],[3],[17],[9],[9],[9],[3],[23],[2],[9],[9],[4],[18],[3],[9],[31],[9],[9],[30],[30],[9],[9],[19],[6],[1],[9],[15],[18],[25],[9],[16],[9],[11],[9],[11],[9],[9],[17],[15],[9],[9],[9],[9],[9],[6],[9],[17],[9],[9],[10],[9],[9],[22],[6],[9],[9],[29],[9],[30],[9],[19],[26],[25],[27],[21],[28],[5],[5],[9],[9],[9],[21],[4],[9],[9],[14],[6],[22],[30],[9],[1],[30],[6],[9],[14],[7],[1],[12],[17],[9],[5],[1],[3],[25],[9],[28],[26],[18],[14],[5],[9],[29],[26],[10],[9],[15],[9],[9],[19],[28],[9],[9],[6],[9],[2],[21],[9],[9],[9],[28],[3],[4],[9],[21],[5],[9],[26],[9],[9],[31],[2],[1],[28],[9],[6],[11],[9],[0],[9],[9],[3],[13],[11],[24],[14],[1],[9],[9],[24],[9],[9],[9],[11],[11],[11],[8],[22],[2],[9],[9],[25],[29],[2],[9],[9],[9],[18],[30],[9],[19],[0],[25],[9],[14],[23],[17],[9],[9],[24],[20],[9],[9],[13],[7],[9],[0],[9],[9],[9],[3],[9],[13],[17],[14],[19],[13],[9],[9],[17],[9],[10],[9],[5],[8],[21],[9],[26],[21],[9],[9],[3],[0],[29],[9],[28],[30],[22],[7],[9],[21],[9],[13],[3],[9],[10],[9],[9],[9],[10],[12],[9],[19],[31],[20],[9],[9],[15],[9],[22],[9],[7],[9],[15]],[[30],[13],[17],[9],[0],[19],[9],[9],[0],[9],[23],[5],[9],[9],[17],[9],[9],[9],[9],[9],[9],[30],[23],[9],[9],[9],[17],[9],[2],[23],[9],[27],[9],[7],[9],[21],[25],[9],[24],[6],[21],[2],[9],[3],[16],[24],[9],[9],[9],[23],[9],[8],[25],[2],[14],[9],[9],[9],[0],[13],[9],[9],[9],[16],[29],[9],[31],[13],[15],[9],[7],[23],[28],[12],[9],[9],[8],[9],[9],[30],[8],[16],[9],[23],[0],[17],[9],[8],[13],[9],[9],[9],[9],[9],[9],[14],[5],[9],[22],[22],[31],[18],[0],[26],[12],[19],[29],[14],[9],[9],[31],[9],[22],[4],[9],[14],[9],[8],[9],[9],[5],[9],[9],[9],[18],[21],[18],[9],[15],[9],[7],[9],[13],[4],[5],[0],[14],[23],[5],[9],[29],[25],[19],[9],[9],[27],[30],[3],[9],[9],[9],[30],[8],[9],[9],[9],[10],[9],[28],[28],[0],[10],[9],[23],[4],[30],[2],[3],[9],[9],[9],[9],[18],[9],[28],[13],[9],[14],[20],[30],[5],[9],[18],[9],[12],[29],[9],[23],[12],[4],[1],[9],[9],[1],[22],[9],[9],[6],[9],[20],[26],[5],[9],[9],[18],[9],[2],[9],[9],[22],[9],[9],[24],[22],[10],[9],[7],[9],[4],[17],[27],[14],[13],[9],[31],[23],[26],[4],[6],[8],[4],[17],[5],[8],[0],[28],[9],[9],[28],[9],[26],[17],[31],[9],[9],[9],[18],[9],[9],[19],[24],[9],[14],[7],[9],[30],[13],[9],[18],[23],[25],[5],[18],[18],[7],[31],[9],[5],[0],[28],[9],[9],[12],[28],[9],[19],[21],[5],[24],[27],[9],[9],[12],[9],[29],[9],[9],[17],[29],[9],[29],[9],[9],[14],[16],[9],[9],[19],[9],[17],[20],[6],[28],[11],[9],[9],[9],[9],[19],[9],[9],[12],[9],[2],[9],[9],[15],[9],[16],[16],[9],[10],[9],[9],[9],[5],[6],[12],[5],[9],[9],[17],[9],[9],[21],[30],[30],[9],[8],[9],[5],[9],[9],[15],[9],[2],[28],[9],[9],[9],[1],[3],[9],[9],[9],[9],[6],[18],[9],[9],[28],[9],[10],[9],[10],[9],[9],[9],[30],[9],[9],[9],[3],[16],[9],[24],[9],[9],[9],[2],[2],[19],[2],[14],[1],[9],[9],[15],[9],[19],[9],[9],[9],[9],[9],[12],[21],[9],[9],[9],[25],[20],[17],[27],[17],[9],[11],[9],[9],[30],[9],[16],[9],[9],[31],[31],[9],[9],[9],[3],[9],[9],[29],[22],[24],[31],[8],[5],[11],[9],[9],[18],[16],[1],[9],[9],[9],[31],[9],[9],[9],[7],[19],[9],[9],[24],[13],[9],[9],[9],[3],[9],[5],[2],[9],[30],[28],[4],[9],[9],[9],[9],[9],[31],[14],[30],[9],[31],[28],[22],[9],[13],[19],[9],[9],[9],[29],[9],[9],[9],[9],[16],[27],[21],[16],[6],[8],[9],[9],[9],[9],[20],[9],[9],[9],[9],[9],[9],[9],[29],[9],[25],[9],[9],[9],[9],[9],[9],[23],[2],[19],[9]],[[12],[11],[10],[13],[13],[14],[28],[10],[29],[18],[5],[25],[6],[8],[9],[3],[13],[29],[9],[9],[25],[6],[9],[11],[9],[11],[9],[8],[9],[9],[9],[24],[9],[27],[9],[18],[28],[21],[12],[0],[9],[4],[9],[0],[9],[6],[9],[28],[9],[0],[13],[26],[7],[20],[3],[10],[4],[3],[18],[0],[20],[14],[5],[22],[9],[9],[4],[16],[10],[9],[9],[9],[9],[9],[9],[15],[29],[9],[5],[9],[24],[31],[31],[6],[3],[16],[9],[27],[28],[29],[9],[17],[9],[3],[25],[28],[25],[24],[26],[5],[27],[9],[9],[13],[9],[28],[31],[9],[9],[0],[28],[9],[9],[9],[9],[9],[26],[9],[10],[9],[6],[11],[9],[20],[17],[21],[9],[9],[13],[27],[9],[9],[9],[31],[9],[23],[16],[9],[18],[17],[9],[21],[17],[14],[7],[9],[22],[20],[9],[10],[9],[9],[21],[5],[9],[9],[9],[30],[14],[17],[21],[10],[9],[17],[9],[9],[9],[22],[4],[0],[24],[9],[9],[1],[29],[21],[26],[12],[20],[9],[24],[9],[9],[9],[22],[29],[3],[9],[9],[24],[23],[23],[7],[29],[9],[16],[9],[9],[9],[0],[4],[11],[15],[23],[29],[5],[20],[25],[9],[17],[9],[13],[9],[9],[20],[26],[9],[9],[9],[9],[9],[9],[9],[9],[27],[9],[25],[22],[9],[9],[9],[26],[2],[21],[21],[9],[24],[20],[26],[29],[9],[9],[31],[7],[9],[18],[0],[9],[1],[23],[9],[20],[15],[8],[14],[27],[9],[8],[9],[26],[9],[16],[21],[9],[9],[30],[17],[29],[19],[9],[31],[6],[9],[7],[9],[17],[14],[0],[9],[11],[5],[7],[9],[9],[9],[5],[15],[8],[9],[9],[26],[9],[10],[9],[5],[17],[24],[2],[10],[9],[9],[9],[30],[12],[9],[1],[9],[28],[9],[11],[11],[2],[9],[27],[9],[9],[19],[9],[9],[3],[9],[28],[9],[26],[24],[9],[9],[9],[19],[7],[26],[10],[31],[9],[13],[9],[24],[2],[9],[14],[30],[6],[25],[21],[19],[18],[10],[9],[9],[4],[9],[28],[24],[9],[9],[29],[16],[28],[9],[5],[9],[1],[9],[9],[28],[18],[9],[9],[6],[9],[0],[2],[8],[30],[22],[14],[9],[9],[5],[5],[2],[9],[5],[17],[9],[3],[9],[24],[9],[8],[16],[12],[3],[9],[23],[7],[10],[9],[3],[9],[9],[31],[9],[9],[16],[27],[9],[22],[3],[4],[12],[9],[21],[9],[9],[9],[26],[4],[9],[9],[3],[30],[8],[9],[9],[1],[9],[9],[2],[19],[4],[16],[25],[31],[13],[24],[24],[9],[6],[9],[12],[21],[2],[9],[9],[10],[9],[9],[18],[22],[9],[12],[9],[20],[9],[11],[0],[9],[9],[7],[9],[9],[9],[9],[26],[20],[9],[6],[9],[9],[3],[26],[9],[9],[31],[22],[27],[4],[9],[18],[10],[0],[23],[9],[9],[9],[9],[8],[9],[9],[25],[15],[30],[7],[24],[12],[27],[9],[9],[10],[9],[13],[9],[9],[27],[9],[6],[23],[9],[23],[2],[9]],[[30],[9],[5],[9],[9],[9],[3],[15],[17],[11],[9],[9],[9],[6],[17],[9],[7],[9],[13],[26],[9],[9],[9],[18],[6],[29],[27],[9],[16],[9],[9],[9],[7],[17],[22],[9],[9],[15],[31],[10],[9],[9],[26],[9],[23],[15],[24],[3],[9],[27],[9],[9],[9],[29],[19],[8],[9],[9],[27],[9],[10],[9],[14],[6],[16],[9],[12],[25],[14],[9],[9],[16],[30],[2],[9],[9],[9],[9],[31],[9],[17],[9],[9],[9],[23],[23],[9],[9],[17],[9],[21],[17],[9],[4],[13],[9],[0],[9],[9],[9],[9],[9],[3],[14],[9],[9],[9],[5],[31],[2],[9],[23],[9],[9],[6],[9],[16],[7],[5],[9],[22],[9],[9],[9],[27],[9],[9],[9],[20],[5],[6],[12],[22],[16],[9],[9],[9],[9],[1],[12],[9],[1],[17],[27],[0],[30],[13],[30],[1],[18],[27],[5],[2],[9],[27],[9],[2],[19],[25],[9],[9],[20],[2],[14],[25],[11],[9],[9],[4],[9],[8],[9],[9],[9],[9],[9],[12],[21],[13],[9],[27],[19],[21],[9],[9],[19],[9],[5],[24],[11],[2],[25],[9],[9],[6],[28],[14],[9],[25],[17],[9],[17],[0],[5],[21],[9],[9],[9],[9],[9],[26],[2],[22],[0],[8],[9],[13],[22],[9],[18],[9],[30],[9],[31],[9],[17],[9],[9],[13],[9],[21],[9],[6],[25],[1],[11],[9],[10],[9],[9],[9],[27],[9],[14],[9],[9],[16],[23],[11],[7],[8],[13],[11],[8],[9],[6],[25],[9],[11],[13],[9],[27],[13],[13],[26],[9],[15],[29],[12],[9],[9],[29],[3],[9],[24],[7],[25],[11],[26],[9],[4],[9],[9],[1],[11],[9],[25],[9],[18],[8],[9],[9],[15],[9],[9],[29],[9],[23],[27],[9],[9],[15],[9],[6],[1],[17],[16],[30],[7],[9],[9],[7],[15],[16],[18],[9],[30],[5],[29],[9],[4],[1],[9],[9],[9],[21],[9],[9],[9],[9],[12],[16],[25],[15],[18],[2],[9],[9],[9],[25],[17],[9],[9],[9],[5],[9],[8],[31],[20],[24],[9],[9],[9],[9],[11],[6],[18],[9],[25],[19],[9],[26],[17],[9],[1],[9],[9],[5],[29],[9],[9],[23],[29],[12],[9],[22],[9],[17],[2],[9],[23],[31],[11],[9],[9],[9],[30],[9],[9],[9],[9],[29],[9],[9],[29],[9],[21],[25],[9],[9],[9],[18],[9],[1],[9],[9],[22],[16],[9],[27],[29],[9],[9],[10],[24],[9],[9],[11],[9],[23],[9],[9],[9],[9],[9],[9],[0],[9],[5],[19],[13],[9],[24],[9],[0],[4],[19],[9],[6],[24],[3],[16],[18],[17],[9],[9],[9],[2],[5],[9],[9],[27],[17],[1],[9],[8],[9],[18],[9],[18],[9],[31],[25],[9],[8],[0],[9],[25],[9],[9],[9],[9],[16],[7],[9],[9],[11],[17],[5],[15],[3],[10],[18],[9],[0],[9],[19],[7],[11],[9],[18],[9],[9],[9],[9],[12],[9],[23],[9],[11],[9],[9],[9],[30],[0],[3],[9],[24],[10],[9],[9],[20]],[[1],[13],[22],[28],[0],[21],[13],[9],[13],[20],[9],[20],[16],[11],[9],[7],[9],[9],[6],[12],[7],[9],[9],[9],[28],[17],[9],[23],[8],[9],[24],[0],[19],[3],[12],[9],[7],[9],[9],[9],[24],[9],[12],[13],[5],[1],[9],[7],[1],[7],[9],[14],[13],[7],[30],[21],[27],[15],[9],[16],[9],[9],[9],[7],[18],[9],[9],[31],[9],[3],[9],[13],[9],[13],[9],[8],[9],[31],[9],[17],[12],[9],[9],[31],[17],[9],[9],[9],[9],[11],[24],[31],[5],[9],[9],[9],[9],[8],[23],[10],[28],[9],[7],[18],[9],[16],[9],[6],[9],[23],[9],[9],[25],[9],[15],[0],[16],[15],[30],[27],[9],[15],[13],[13],[19],[18],[9],[21],[9],[7],[9],[9],[7],[9],[10],[5],[30],[6],[9],[16],[9],[17],[9],[9],[9],[7],[10],[9],[9],[18],[9],[22],[9],[11],[9],[9],[9],[14],[30],[22],[8],[10],[9],[11],[9],[18],[10],[16],[1],[9],[28],[9],[10],[2],[24],[9],[28],[9],[3],[9],[9],[9],[8],[9],[9],[9],[30],[10],[9],[9],[9],[23],[9],[9],[2],[26],[25],[21],[19],[9],[5],[9],[9],[26],[9],[17],[9],[8],[0],[9],[14],[5],[10],[29],[9],[4],[9],[22],[29],[20],[9],[31],[8],[26],[9],[30],[10],[22],[18],[2],[5],[9],[9],[9],[8],[9],[9],[13],[9],[21],[27],[9],[14],[3],[1],[9],[4],[6],[6],[22],[9],[9],[22],[9],[0],[4],[9],[20],[4],[4],[10],[9],[23],[9],[5],[22],[26],[9],[9],[16],[2],[18],[9],[29],[12],[10],[20],[8],[7],[7],[9],[4],[29],[9],[11],[16],[9],[4],[8],[9],[9],[9],[5],[9],[3],[15],[24],[24],[9],[31],[31],[1],[3],[9],[23],[28],[6],[31],[9],[9],[12],[22],[24],[9],[17],[31],[9],[9],[9],[18],[25],[9],[9],[9],[9],[9],[26],[17],[30],[9],[9],[9],[14],[9],[9],[9],[19],[4],[20],[25],[3],[2],[9],[9],[9],[21],[9],[9],[8],[31],[9],[22],[14],[9],[9],[9],[9],[5],[30],[9],[9],[12],[20],[1],[6],[28],[9],[1],[6],[25],[9],[26],[11],[31],[9],[9],[5],[9],[18],[14],[9],[9],[9],[9],[9],[19],[9],[9],[9],[9],[18],[3],[9],[9],[15],[9],[17],[26],[9],[31],[22],[16],[27],[8],[15],[26],[9],[13],[4],[5],[27],[21],[9],[20],[9],[8],[27],[4],[14],[17],[9],[9],[11],[5],[15],[9],[9],[7],[24],[7],[9],[9],[9],[13],[9],[9],[23],[9],[9],[26],[9],[9],[30],[10],[8],[26],[9],[6],[9],[30],[29],[19],[9],[9],[10],[16],[27],[7],[9],[22],[9],[9],[23],[8],[22],[16],[20],[9],[4],[25],[11],[9],[9],[15],[9],[8],[15],[24],[29],[13],[9],[9],[9],[4],[8],[9],[3],[9],[9],[13],[9],[6],[9],[9],[9],[11],[9],[17],[21],[17],[1],[23],[9],[2],[9],[9],[28],[20],[26],[31],[22],[16]],[[23],[30],[9],[9],[9],[9],[9],[5],[9],[20],[9],[19],[21],[9],[9],[9],[3],[25],[27],[15],[9],[14],[15],[19],[26],[9],[23],[9],[9],[9],[9],[9],[9],[9],[31],[9],[9],[9],[9],[13],[18],[8],[9],[9],[22],[31],[9],[9],[17],[10],[9],[21],[9],[4],[12],[24],[22],[13],[9],[9],[9],[10],[9],[9],[26],[9],[9],[12],[9],[8],[15],[0],[9],[18],[9],[9],[16],[11],[24],[9],[18],[26],[7],[7],[9],[9],[9],[9],[9],[0],[13],[21],[9],[25],[17],[25],[1],[29],[9],[4],[9],[28],[23],[9],[26],[9],[4],[9],[9],[9],[31],[9],[25],[27],[5],[6],[18],[13],[5],[8],[9],[9],[19],[11],[13],[9],[10],[16],[9],[26],[9],[9],[19],[25],[9],[14],[6],[17],[6],[9],[9],[16],[9],[5],[28],[25],[17],[9],[18],[18],[20],[9],[6],[9],[18],[5],[9],[25],[16],[9],[9],[9],[9],[9],[9],[18],[9],[9],[25],[2],[12],[15],[9],[9],[23],[13],[17],[15],[9],[26],[9],[9],[4],[24],[10],[18],[22],[9],[28],[26],[27],[0],[31],[20],[3],[9],[9],[21],[28],[9],[9],[9],[9],[3],[4],[9],[0],[9],[16],[4],[26],[9],[2],[28],[7],[9],[12],[5],[27],[13],[8],[8],[28],[9],[9],[9],[12],[9],[9],[9],[22],[9],[9],[30],[20],[9],[9],[9],[27],[12],[9],[9],[15],[24],[29],[9],[9],[24],[10],[27],[9],[6],[9],[25],[9],[26],[9],[13],[9],[9],[9],[1],[18],[21],[18],[11],[9],[9],[26],[19],[2],[10],[31],[9],[8],[9],[23],[23],[31],[2],[9],[9],[2],[9],[9],[8],[9],[30],[9],[16],[3],[9],[14],[9],[24],[9],[9],[9],[9],[9],[3],[9],[9],[24],[14],[31],[31],[9],[9],[21],[20],[0],[29],[16],[9],[9],[9],[9],[7],[9],[9],[9],[12],[9],[29],[21],[6],[16],[7],[29],[9],[9],[9],[9],[9],[7],[0],[31],[9],[18],[9],[11],[9],[9],[25],[17],[3],[0],[11],[9],[9],[9],[9],[13],[9],[9],[14],[5],[20],[31],[2],[9],[9],[0],[3],[9],[28],[28],[9],[14],[20],[9],[2],[9],[9],[16],[3],[1],[9],[9],[21],[18],[9],[9],[30],[9],[9],[9],[9],[20],[9],[9],[5],[29],[9],[29],[9],[15],[30],[24],[9],[9],[9],[13],[9],[9],[10],[9],[9],[9],[18],[3],[11],[9],[2],[10],[9],[31],[2],[24],[9],[27],[4],[14],[12],[10],[29],[9],[25],[30],[3],[4],[9],[6],[13],[9],[9],[2],[9],[6],[26],[9],[9],[9],[9],[9],[17],[12],[12],[17],[22],[29],[31],[9],[9],[7],[9],[9],[9],[2],[9],[0],[9],[9],[9],[24],[9],[12],[26],[0],[19],[25],[27],[3],[9],[9],[19],[4],[16],[9],[6],[27],[9],[1],[18],[9],[9],[9],[9],[11],[17],[19],[25],[19],[28],[22],[29],[2],[5],[19],[9],[15],[27],[9],[2],[9],[9],[9],[9],[9],[4],[22]],[[1],[9],[9],[17],[24],[9],[6],[9],[9],[9],[21],[17],[9],[9],[9],[3],[9],[9],[28],[13],[28],[9],[9],[23],[9],[4],[21],[13],[14],[0],[9],[16],[2],[11],[9],[9],[26],[21],[9],[9],[9],[5],[5],[21],[8],[9],[12],[30],[14],[9],[9],[9],[6],[9],[12],[9],[24],[9],[0],[9],[9],[9],[20],[23],[16],[9],[12],[9],[9],[9],[9],[9],[9],[4],[9],[9],[11],[9],[14],[26],[13],[26],[0],[22],[9],[16],[13],[9],[4],[28],[30],[9],[9],[29],[9],[9],[1],[9],[0],[9],[13],[25],[19],[9],[13],[4],[8],[9],[13],[9],[8],[19],[22],[8],[8],[5],[9],[3],[9],[15],[28],[9],[9],[9],[20],[2],[12],[9],[9],[17],[27],[9],[16],[9],[9],[9],[26],[9],[20],[9],[9],[9],[9],[29],[18],[22],[9],[26],[9],[3],[26],[29],[20],[9],[9],[9],[15],[10],[11],[23],[9],[9],[12],[3],[9],[25],[15],[22],[22],[1],[9],[13],[9],[9],[18],[9],[11],[9],[8],[23],[14],[6],[6],[9],[18],[9],[11],[9],[9],[9],[11],[13],[9],[9],[19],[9],[9],[21],[2],[9],[30],[1],[3],[25],[16],[14],[28],[9],[9],[1],[9],[9],[9],[29],[0],[9],[26],[15],[9],[9],[18],[7],[9],[17],[9],[24],[9],[16],[20],[8],[29],[25],[9],[17],[16],[9],[9],[17],[16],[21],[4],[9],[28],[16],[3],[9],[9],[6],[9],[5],[9],[19],[28],[29],[0],[6],[16],[9],[21],[24],[9],[9],[21],[23],[25],[17],[16],[9],[9],[9],[3],[21],[11],[9],[19],[19],[9],[1],[9],[9],[6],[19],[0],[9],[9],[9],[6],[9],[15],[19],[28],[9],[9],[9],[2],[30],[16],[9],[9],[20],[11],[12],[16],[14],[9],[9],[12],[10],[9],[22],[8],[26],[9],[9],[9],[9],[0],[10],[24],[30],[11],[9],[16],[27],[9],[9],[9],[21],[11],[1],[9],[9],[22],[0],[10],[9],[27],[9],[9],[24],[23],[9],[12],[5],[9],[21],[29],[6],[0],[29],[9],[1],[9],[12],[9],[9],[30],[9],[9],[9],[3],[22],[9],[9],[9],[5],[9],[9],[27],[19],[2],[5],[11],[0],[9],[19],[9],[9],[8],[9],[23],[9],[9],[16],[9],[21],[9],[9],[18],[10],[9],[9],[3],[9],[9],[9],[21],[27],[24],[9],[24],[9],[9],[9],[26],[9],[8],[11],[16],[30],[28],[9],[9],[9],[9],[9],[24],[2],[9],[27],[1],[9],[9],[19],[10],[23],[9],[13],[0],[9],[29],[31],[12],[11],[26],[9],[9],[9],[15],[5],[9],[30],[6],[9],[9],[9],[31],[9],[9],[24],[9],[2],[9],[1],[21],[22],[11],[30],[9],[8],[25],[9],[24],[8],[9],[2],[9],[9],[4],[13],[17],[9],[21],[30],[3],[26],[9],[9],[4],[19],[19],[17],[9],[16],[9],[9],[9],[9],[9],[0],[6],[7],[9],[9],[9],[9],[3],[9],[19],[9],[6],[12],[9],[9],[20],[22],[20],[18],[9],[3],[9],[3]],[[9],[25],[13],[9],[22],[9],[9],[9],[27],[4],[9],[28],[26],[29],[7],[11],[23],[9],[14],[9],[14],[11],[11],[9],[4],[25],[9],[9],[27],[1],[1],[9],[9],[9],[21],[9],[13],[0],[9],[24],[9],[8],[9],[9],[23],[11],[30],[8],[14],[14],[17],[26],[2],[1],[9],[9],[26],[9],[9],[12],[9],[5],[9],[21],[9],[29],[14],[9],[26],[4],[9],[22],[26],[26],[9],[9],[28],[9],[18],[29],[30],[23],[9],[22],[9],[31],[25],[3],[1],[23],[1],[9],[9],[21],[25],[2],[9],[9],[22],[9],[9],[9],[21],[9],[9],[9],[9],[10],[9],[2],[9],[14],[9],[23],[2],[9],[9],[13],[9],[27],[9],[9],[21],[30],[1],[0],[9],[4],[7],[3],[16],[6],[16],[19],[9],[24],[8],[7],[13],[14],[17],[2],[21],[9],[12],[9],[10],[28],[9],[30],[18],[24],[9],[3],[29],[27],[9],[9],[9],[16],[23],[11],[17],[9],[9],[21],[30],[9],[9],[9],[3],[20],[19],[29],[6],[9],[23],[9],[9],[9],[18],[9],[9],[9],[9],[16],[11],[20],[9],[9],[10],[30],[9],[9],[2],[9],[31],[1],[17],[13],[29],[3],[16],[9],[9],[9],[3],[10],[9],[9],[19],[9],[9],[6],[9],[27],[9],[9],[9],[22],[9],[9],[22],[9],[14],[9],[9],[16],[24],[9],[17],[7],[9],[9],[9],[9],[9],[9],[27],[1],[10],[3],[29],[1],[27],[3],[9],[9],[25],[9],[25],[26],[9],[17],[9],[22],[19],[9],[9],[28],[9],[26],[9],[9],[3],[9],[6],[12],[23],[9],[10],[20],[9],[9],[0],[13],[3],[7],[9],[29],[6],[0],[9],[9],[11],[6],[20],[9],[9],[19],[9],[9],[9],[9],[28],[9],[6],[9],[23],[12],[9],[4],[5],[1],[9],[4],[29],[9],[6],[9],[23],[9],[6],[2],[9],[15],[9],[9],[7],[9],[9],[6],[9],[9],[9],[31],[0],[23],[9],[9],[1],[16],[7],[9],[8],[9],[13],[25],[9],[7],[9],[8],[18],[29],[9],[14],[9],[6],[9],[8],[9],[9],[9],[9],[9],[9],[9],[9],[31],[24],[31],[4],[9],[26],[9],[28],[15],[9],[26],[15],[13],[9],[9],[9],[28],[9],[6],[10],[9],[9],[9],[8],[3],[21],[9],[25],[9],[9],[9],[9],[3],[29],[28],[9],[9],[9],[9],[9],[29],[9],[9],[25],[12],[9],[6],[9],[9],[21],[0],[28],[1],[9],[9],[10],[16],[19],[17],[9],[19],[19],[9],[0],[9],[9],[21],[11],[9],[31],[9],[4],[31],[20],[22],[9],[0],[9],[14],[9],[22],[9],[9],[9],[9],[21],[9],[9],[0],[25],[16],[9],[14],[0],[9],[20],[9],[9],[10],[26],[29],[9],[8],[27],[9],[24],[3],[23],[1],[9],[19],[5],[25],[29],[9],[5],[0],[9],[28],[9],[9],[9],[5],[19],[17],[30],[21],[11],[4],[15],[3],[9],[29],[25],[9],[9],[8],[5],[9],[25],[15],[27],[21],[9],[9],[9],[1],[13],[23],[9],[8],[9],[9],[11]],[[5],[24],[4],[9],[19],[15],[7],[2],[20],[25],[9],[9],[9],[1],[9],[17],[17],[9],[13],[9],[24],[9],[6],[13],[25],[9],[25],[9],[10],[9],[9],[29],[9],[31],[11],[9],[0],[25],[12],[9],[9],[4],[9],[9],[25],[9],[19],[9],[25],[30],[9],[9],[9],[29],[13],[9],[30],[8],[0],[15],[9],[9],[9],[3],[30],[9],[9],[28],[9],[14],[22],[2],[9],[5],[13],[9],[11],[22],[30],[19],[10],[12],[9],[26],[9],[1],[11],[9],[9],[22],[9],[22],[8],[3],[19],[30],[23],[4],[7],[19],[25],[9],[9],[26],[9],[27],[28],[14],[19],[9],[9],[9],[9],[9],[13],[9],[4],[9],[6],[23],[9],[9],[0],[12],[9],[9],[12],[25],[17],[22],[17],[9],[9],[2],[9],[9],[21],[0],[26],[8],[31],[17],[20],[3],[20],[9],[9],[9],[9],[5],[29],[30],[9],[2],[9],[29],[9],[19],[9],[9],[9],[27],[7],[1],[9],[9],[31],[5],[8],[9],[26],[9],[18],[22],[9],[9],[9],[5],[9],[31],[2],[29],[2],[6],[9],[9],[9],[9],[9],[18],[0],[22],[29],[9],[9],[28],[26],[31],[4],[21],[25],[29],[9],[9],[9],[29],[9],[11],[9],[26],[9],[19],[22],[9],[24],[24],[15],[12],[9],[9],[30],[6],[0],[25],[12],[29],[14],[27],[11],[9],[29],[21],[15],[23],[31],[9],[9],[9],[29],[0],[9],[9],[9],[9],[9],[8],[26],[9],[9],[30],[9],[9],[9],[9],[6],[15],[28],[5],[16],[29],[24],[27],[9],[3],[11],[3],[25],[23],[10],[9],[9],[9],[9],[24],[20],[21],[12],[0],[9],[9],[25],[22],[9],[22],[3],[9],[29],[11],[9],[9],[8],[29],[4],[9],[9],[9],[9],[16],[9],[9],[9],[9],[26],[11],[9],[7],[13],[24],[16],[11],[20],[9],[9],[9],[23],[9],[18],[18],[9],[9],[9],[0],[17],[16],[23],[28],[4],[9],[9],[15],[6],[12],[9],[9],[18],[1],[9],[9],[9],[8],[29],[9],[9],[3],[4],[10],[9],[9],[9],[9],[14],[9],[17],[9],[5],[16],[0],[9],[7],[9],[26],[29],[16],[15],[9],[9],[21],[9],[9],[7],[0],[20],[11],[9],[4],[2],[22],[9],[4],[9],[15],[14],[10],[2],[9],[29],[29],[19],[20],[8],[2],[29],[12],[16],[9],[9],[0],[9],[27],[31],[24],[9],[26],[14],[17],[28],[9],[9],[6],[20],[8],[14],[22],[23],[22],[25],[9],[16],[15],[25],[9],[6],[9],[8],[17],[9],[4],[29],[9],[27],[9],[9],[31],[31],[20],[9],[9],[13],[9],[9],[9],[9],[9],[9],[9],[7],[9],[6],[9],[9],[22],[9],[6],[9],[23],[9],[21],[9],[5],[9],[10],[9],[24],[9],[0],[9],[19],[24],[12],[29],[27],[9],[9],[11],[16],[13],[9],[8],[9],[6],[26],[24],[22],[23],[9],[13],[13],[30],[6],[9],[24],[9],[9],[22],[2],[5],[9],[9],[9],[9],[19],[9],[30],[29],[9],[9],[25],[23],[15],[10],[9],[5]],[[9],[9],[9],[12],[22],[11],[9],[9],[18],[9],[18],[9],[20],[9],[9],[3],[9],[17],[16],[9],[9],[9],[9],[2],[9],[15],[9],[23],[31],[7],[9],[8],[9],[9],[21],[9],[9],[9],[9],[20],[31],[9],[8],[9],[9],[9],[9],[14],[14],[9],[24],[14],[9],[9],[2],[28],[7],[9],[9],[9],[9],[3],[26],[23],[4],[14],[15],[15],[20],[17],[9],[9],[26],[9],[29],[8],[9],[9],[15],[9],[20],[26],[29],[9],[29],[12],[9],[29],[21],[9],[11],[26],[27],[9],[22],[15],[25],[25],[10],[16],[11],[6],[13],[28],[3],[9],[9],[11],[20],[6],[15],[9],[5],[2],[9],[11],[18],[9],[1],[9],[9],[10],[1],[9],[9],[9],[11],[9],[9],[9],[4],[9],[15],[9],[29],[9],[9],[9],[9],[29],[10],[9],[23],[9],[29],[9],[0],[6],[6],[9],[16],[9],[9],[9],[9],[9],[9],[23],[9],[5],[9],[9],[22],[26],[9],[13],[5],[9],[29],[17],[9],[9],[26],[28],[9],[21],[3],[14],[9],[7],[20],[9],[20],[26],[1],[9],[6],[13],[9],[9],[9],[0],[5],[9],[23],[19],[9],[27],[23],[9],[27],[9],[20],[9],[0],[9],[9],[21],[2],[10],[22],[4],[9],[30],[1],[9],[23],[9],[9],[19],[9],[9],[16],[3],[9],[9],[10],[21],[9],[21],[1],[16],[9],[29],[13],[9],[9],[6],[6],[27],[9],[14],[9],[9],[9],[11],[9],[9],[23],[9],[2],[28],[9],[9],[18],[9],[9],[21],[21],[1],[9],[9],[9],[13],[9],[17],[12],[9],[9],[2],[12],[9],[9],[28],[9],[9],[25],[14],[0],[18],[9],[11],[9],[9],[9],[5],[31],[9],[17],[20],[18],[9],[22],[5],[16],[9],[9],[4],[9],[9],[9],[2],[7],[13],[9],[9],[5],[9],[1],[7],[28],[3],[28],[15],[26],[9],[14],[20],[1],[25],[26],[20],[9],[0],[10],[9],[9],[16],[9],[30],[9],[30],[18],[9],[27],[24],[11],[27],[7],[27],[9],[26],[31],[8],[29],[9],[9],[9],[9],[9],[7],[23],[9],[9],[7],[9],[9],[6],[25],[13],[3],[9],[26],[9],[9],[9],[19],[9],[27],[4],[9],[9],[19],[9],[9],[9],[17],[9],[21],[29],[5],[19],[4],[6],[3],[9],[9],[9],[19],[26],[8],[26],[2],[9],[17],[24],[13],[9],[2],[4],[9],[9],[24],[9],[30],[2],[20],[16],[9],[9],[9],[9],[26],[9],[9],[13],[17],[10],[2],[16],[9],[9],[9],[2],[14],[9],[5],[8],[9],[9],[9],[22],[9],[14],[26],[26],[25],[9],[29],[11],[21],[5],[16],[9],[20],[9],[9],[31],[28],[9],[4],[30],[27],[12],[9],[10],[24],[16],[17],[13],[9],[1],[21],[3],[9],[9],[12],[9],[13],[16],[19],[9],[9],[9],[9],[25],[7],[9],[9],[9],[24],[9],[25],[12],[21],[13],[25],[0],[3],[9],[9],[21],[9],[19],[5],[9],[9],[19],[31],[13],[9],[5],[28],[1],[9],[16],[29],[14],[29],[3],[9],[3]],[[28],[1],[9],[7],[0],[15],[10],[9],[9],[28],[29],[9],[16],[9],[3],[14],[9],[9],[17],[25],[9],[9],[9],[16],[15],[10],[8],[9],[26],[9],[9],[14],[28],[8],[9],[9],[7],[9],[28],[9],[9],[5],[23],[9],[3],[21],[28],[0],[23],[9],[9],[24],[23],[19],[29],[14],[25],[6],[19],[9],[9],[23],[9],[9],[12],[9],[9],[15],[16],[9],[2],[26],[27],[9],[2],[9],[27],[19],[2],[15],[9],[31],[18],[9],[9],[15],[14],[12],[9],[28],[21],[13],[25],[9],[9],[9],[9],[3],[9],[9],[24],[11],[27],[9],[9],[9],[31],[1],[17],[9],[9],[4],[9],[9],[12],[16],[9],[20],[9],[21],[31],[22],[4],[9],[10],[19],[19],[9],[27],[9],[24],[9],[24],[9],[20],[16],[9],[9],[3],[8],[16],[29],[9],[17],[15],[14],[21],[9],[9],[3],[9],[26],[9],[24],[8],[29],[7],[15],[28],[9],[26],[28],[13],[22],[10],[4],[7],[9],[9],[9],[18],[11],[6],[9],[21],[12],[9],[10],[21],[12],[9],[18],[10],[4],[1],[25],[25],[9],[4],[9],[9],[9],[9],[24],[9],[9],[22],[5],[23],[31],[1],[9],[9],[20],[30],[9],[27],[1],[21],[9],[9],[8],[22],[10],[14],[28],[9],[23],[9],[9],[9],[6],[13],[26],[11],[27],[20],[9],[9],[1],[9],[13],[20],[9],[13],[9],[27],[9],[9],[4],[24],[7],[0],[9],[17],[7],[4],[31],[15],[6],[2],[12],[9],[23],[16],[2],[26],[9],[9],[18],[7],[31],[16],[9],[9],[9],[16],[9],[5],[7],[13],[9],[9],[9],[9],[22],[22],[9],[10],[28],[9],[18],[13],[9],[9],[22],[19],[5],[29],[7],[21],[9],[9],[2],[14],[0],[19],[25],[11],[6],[9],[19],[9],[26],[9],[9],[17],[23],[15],[9],[26],[29],[9],[30],[9],[9],[9],[9],[14],[9],[9],[17],[0],[13],[4],[16],[9],[9],[15],[0],[12],[9],[5],[9],[25],[9],[19],[16],[13],[23],[9],[16],[6],[9],[25],[10],[9],[6],[11],[9],[9],[9],[9],[9],[9],[9],[5],[9],[28],[1],[9],[9],[4],[9],[9],[9],[29],[9],[30],[16],[9],[20],[24],[30],[9],[9],[9],[9],[19],[28],[30],[27],[9],[15],[17],[9],[6],[9],[9],[17],[9],[9],[9],[9],[18],[9],[23],[27],[9],[9],[12],[3],[0],[3],[9],[9],[9],[9],[21],[9],[9],[26],[6],[9],[2],[9],[12],[31],[26],[9],[18],[9],[13],[27],[21],[9],[9],[9],[9],[9],[2],[24],[7],[9],[9],[9],[15],[13],[22],[9],[9],[5],[8],[9],[22],[31],[0],[11],[9],[0],[26],[6],[6],[29],[1],[3],[9],[9],[9],[9],[24],[9],[10],[9],[25],[9],[9],[7],[5],[9],[9],[8],[16],[23],[9],[5],[7],[13],[26],[9],[4],[9],[15],[9],[11],[28],[26],[6],[9],[31],[1],[9],[18],[7],[9],[23],[10],[9],[9],[9],[8],[14],[9],[11],[24],[18],[9],[9],[9],[18],[9],[2]],[[9],[25],[9],[9],[2],[9],[18],[24],[9],[9],[9],[9],[6],[1],[11],[1],[29],[8],[12],[31],[9],[22],[9],[13],[19],[9],[9],[23],[9],[9],[2],[9],[20],[11],[20],[9],[26],[27],[9],[9],[22],[19],[9],[9],[9],[9],[9],[5],[25],[9],[7],[23],[0],[6],[9],[9],[9],[26],[3],[9],[9],[26],[3],[9],[9],[9],[27],[10],[21],[9],[9],[24],[9],[12],[29],[9],[9],[2],[31],[9],[12],[26],[9],[9],[9],[9],[9],[10],[28],[28],[13],[9],[23],[9],[9],[9],[9],[9],[9],[9],[3],[9],[22],[9],[29],[14],[9],[9],[7],[9],[17],[23],[7],[7],[8],[9],[1],[10],[5],[9],[9],[13],[9],[1],[19],[14],[10],[22],[20],[9],[6],[9],[13],[16],[9],[0],[18],[22],[7],[9],[9],[9],[20],[17],[25],[8],[9],[9],[13],[9],[9],[9],[9],[9],[16],[9],[23],[10],[9],[0],[0],[9],[18],[11],[11],[31],[9],[29],[26],[9],[25],[9],[9],[9],[20],[9],[24],[6],[17],[9],[2],[9],[24],[9],[24],[30],[17],[8],[8],[16],[7],[2],[9],[15],[9],[9],[21],[14],[9],[9],[9],[17],[2],[16],[26],[18],[8],[10],[8],[28],[9],[9],[14],[22],[17],[16],[9],[9],[9],[1],[24],[26],[9],[14],[9],[25],[12],[18],[21],[9],[18],[9],[10],[9],[17],[7],[9],[1],[12],[4],[23],[10],[9],[9],[31],[9],[22],[26],[9],[9],[9],[3],[8],[2],[21],[21],[24],[20],[9],[9],[4],[1],[9],[30],[0],[7],[23],[9],[12],[9],[16],[10],[9],[9],[9],[9],[22],[9],[9],[9],[30],[9],[9],[9],[2],[9],[8],[14],[25],[6],[9],[9],[9],[27],[9],[15],[9],[9],[28],[22],[3],[9],[9],[10],[9],[9],[4],[9],[9],[24],[26],[16],[9],[9],[4],[9],[9],[30],[9],[12],[23],[14],[14],[30],[9],[3],[29],[9],[19],[25],[9],[9],[9],[3],[9],[16],[23],[0],[7],[9],[9],[9],[19],[3],[25],[14],[7],[9],[12],[27],[15],[9],[20],[9],[27],[9],[9],[13],[24],[22],[27],[9],[6],[31],[9],[24],[17],[9],[9],[9],[28],[9],[9],[9],[9],[9],[19],[16],[11],[9],[9],[16],[9],[20],[9],[9],[4],[8],[4],[0],[9],[17],[9],[2],[9],[9],[9],[24],[7],[22],[28],[17],[1],[9],[1],[1],[11],[20],[12],[19],[4],[7],[17],[9],[16],[14],[14],[22],[9],[27],[9],[13],[8],[21],[9],[5],[9],[22],[28],[9],[2],[9],[9],[9],[13],[9],[4],[30],[9],[9],[9],[9],[9],[9],[16],[15],[9],[9],[9],[19],[9],[5],[9],[9],[31],[9],[9],[13],[9],[27],[9],[26],[12],[9],[9],[9],[23],[23],[29],[31],[0],[27],[31],[10],[9],[9],[10],[28],[9],[9],[20],[24],[9],[23],[10],[2],[14],[14],[9],[30],[7],[22],[6],[3],[20],[19],[9],[9],[9],[29],[16],[9],[22],[9],[9],[9],[12],[9],[30],[9],[17],[16]],[[3],[9],[30],[9],[9],[9],[29],[9],[18],[9],[9],[0],[9],[30],[30],[23],[3],[5],[9],[10],[7],[9],[9],[7],[9],[17],[9],[3],[27],[15],[9],[18],[9],[20],[9],[0],[9],[9],[9],[0],[23],[9],[23],[2],[9],[1],[19],[9],[15],[11],[4],[10],[9],[21],[9],[9],[17],[3],[9],[9],[22],[19],[9],[9],[9],[1],[9],[20],[12],[9],[22],[6],[9],[12],[9],[4],[9],[9],[9],[29],[3],[4],[29],[30],[30],[9],[6],[17],[9],[27],[7],[7],[9],[15],[8],[9],[6],[30],[16],[12],[9],[27],[5],[9],[9],[9],[18],[16],[9],[9],[19],[29],[0],[19],[9],[1],[1],[10],[24],[22],[9],[8],[12],[30],[13],[19],[6],[9],[0],[8],[23],[29],[9],[9],[9],[9],[14],[9],[9],[1],[31],[9],[24],[10],[0],[9],[18],[22],[12],[23],[28],[20],[30],[9],[5],[24],[9],[9],[4],[19],[26],[9],[9],[22],[23],[9],[15],[9],[9],[18],[9],[2],[8],[26],[9],[7],[2],[14],[2],[9],[9],[28],[21],[9],[9],[19],[8],[9],[6],[22],[26],[9],[29],[14],[18],[31],[5],[9],[9],[0],[9],[17],[17],[19],[11],[11],[5],[2],[17],[15],[9],[9],[9],[4],[9],[15],[12],[9],[17],[9],[24],[30],[9],[9],[9],[9],[12],[27],[9],[9],[1],[6],[9],[24],[27],[9],[16],[9],[24],[8],[9],[8],[26],[9],[9],[9],[12],[9],[9],[9],[9],[9],[20],[9],[14],[20],[9],[22],[2],[14],[3],[13],[20],[1],[18],[9],[5],[4],[9],[2],[15],[28],[9],[13],[25],[14],[10],[30],[0],[27],[9],[1],[2],[9],[17],[22],[9],[7],[31],[16],[0],[9],[4],[28],[9],[2],[9],[9],[29],[9],[4],[9],[19],[15],[24],[0],[20],[9],[4],[9],[9],[16],[11],[9],[17],[8],[9],[9],[9],[9],[9],[18],[9],[9],[5],[2],[9],[9],[9],[9],[9],[9],[29],[5],[0],[25],[9],[9],[23],[14],[28],[4],[9],[9],[9],[14],[9],[9],[18],[9],[20],[13],[9],[30],[2],[14],[31],[1],[9],[9],[23],[9],[22],[22],[9],[11],[26],[28],[24],[9],[9],[21],[9],[11],[11],[9],[12],[28],[17],[17],[25],[24],[18],[12],[22],[14],[21],[17],[9],[22],[2],[28],[28],[30],[24],[5],[9],[25],[1],[19],[4],[9],[9],[17],[9],[9],[24],[9],[6],[24],[9],[3],[9],[9],[2],[9],[13],[9],[9],[29],[1],[0],[23],[29],[20],[9],[9],[9],[9],[0],[0],[4],[28],[12],[9],[26],[9],[9],[19],[9],[5],[9],[9],[9],[27],[9],[14],[9],[17],[14],[22],[9],[9],[31],[9],[9],[5],[20],[4],[24],[28],[15],[9],[14],[10],[31],[9],[29],[9],[30],[21],[9],[5],[25],[23],[4],[9],[27],[28],[9],[16],[3],[9],[9],[9],[9],[1],[16],[23],[20],[14],[21],[9],[31],[9],[9],[9],[24],[9],[17],[18],[9],[9],[5],[9],[18],[9],[17],[2],[7],[26],[31]],[[9],[31],[9],[9],[2],[25],[23],[9],[9],[24],[18],[26],[4],[9],[9],[9],[9],[22],[13],[14],[0],[9],[9],[9],[27],[25],[14],[16],[30],[9],[9],[9],[9],[7],[24],[22],[19],[8],[11],[9],[9],[9],[9],[19],[19],[4],[9],[9],[27],[9],[9],[9],[27],[3],[6],[31],[29],[9],[26],[27],[16],[13],[16],[1],[9],[9],[9],[15],[9],[9],[23],[9],[14],[9],[3],[9],[26],[7],[9],[9],[9],[9],[20],[9],[9],[9],[2],[9],[31],[19],[9],[0],[14],[20],[7],[9],[0],[5],[26],[9],[20],[9],[4],[9],[9],[10],[20],[8],[9],[23],[5],[9],[9],[9],[9],[9],[9],[9],[12],[9],[9],[9],[14],[9],[10],[31],[9],[9],[30],[9],[9],[6],[5],[9],[23],[9],[12],[8],[9],[25],[16],[16],[24],[1],[9],[17],[10],[21],[30],[30],[27],[21],[26],[0],[9],[2],[26],[9],[9],[9],[29],[9],[9],[9],[20],[9],[9],[2],[16],[28],[9],[9],[9],[3],[6],[9],[0],[9],[9],[9],[0],[10],[0],[14],[9],[9],[5],[9],[23],[28],[2],[12],[10],[9],[9],[25],[20],[21],[22],[9],[5],[23],[14],[9],[9],[22],[9],[25],[23],[6],[9],[22],[8],[9],[9],[9],[4],[9],[9],[3],[9],[10],[1],[9],[9],[19],[29],[28],[9],[6],[18],[13],[19],[9],[9],[4],[7],[30],[12],[17],[9],[9],[19],[9],[9],[1],[10],[13],[15],[11],[30],[20],[30],[9],[3],[9],[29],[15],[22],[9],[9],[22],[18],[24],[15],[9],[12],[16],[5],[1],[26],[21],[5],[10],[9],[9],[17],[1],[22],[9],[5],[5],[11],[0],[26],[9],[9],[9],[1],[2],[9],[9],[9],[20],[9],[11],[28],[20],[14],[5],[25],[16],[9],[14],[9],[0],[21],[17],[21],[16],[9],[14],[30],[9],[8],[28],[9],[12],[8],[25],[4],[16],[9],[30],[0],[9],[2],[24],[28],[30],[4],[9],[22],[3],[1],[9],[22],[19],[5],[9],[19],[9],[9],[9],[30],[17],[9],[9],[31],[9],[30],[20],[1],[18],[2],[7],[9],[7],[9],[9],[7],[9],[9],[2],[9],[9],[4],[9],[3],[27],[9],[6],[9],[9],[2],[9],[9],[8],[9],[9],[11],[4],[19],[9],[9],[9],[9],[9],[9],[11],[25],[9],[9],[30],[0],[8],[9],[9],[18],[10],[9],[10],[9],[14],[11],[9],[9],[9],[28],[1],[23],[28],[29],[9],[19],[9],[9],[9],[11],[9],[9],[15],[31],[23],[14],[9],[9],[4],[9],[9],[13],[9],[28],[16],[9],[18],[9],[9],[23],[21],[9],[10],[9],[9],[27],[9],[6],[4],[7],[9],[25],[7],[1],[9],[12],[29],[31],[29],[5],[9],[7],[9],[9],[9],[12],[6],[4],[7],[1],[14],[9],[22],[12],[25],[10],[21],[4],[2],[24],[31],[9],[20],[24],[9],[9],[9],[28],[9],[25],[9],[22],[28],[9],[1],[11],[20],[27],[9],[9],[9],[10],[30],[25],[10],[9],[10],[9],[9],[9],[9],[22],[6]],[[9],[19],[0],[22],[5],[8],[5],[20],[9],[13],[12],[13],[7],[17],[15],[9],[9],[30],[3],[23],[26],[29],[9],[18],[7],[2],[9],[26],[9],[7],[5],[11],[9],[9],[9],[9],[31],[9],[9],[30],[12],[5],[9],[1],[9],[18],[9],[14],[24],[23],[4],[9],[21],[9],[9],[9],[0],[9],[9],[21],[26],[21],[9],[9],[22],[9],[11],[9],[9],[9],[9],[3],[6],[18],[5],[12],[9],[27],[9],[9],[23],[9],[9],[31],[9],[29],[9],[12],[9],[10],[9],[9],[9],[9],[9],[18],[9],[9],[23],[23],[9],[26],[29],[9],[9],[9],[4],[4],[9],[18],[9],[9],[11],[1],[9],[9],[27],[12],[9],[9],[3],[9],[6],[13],[9],[20],[9],[9],[15],[9],[3],[9],[17],[7],[29],[6],[9],[16],[1],[21],[14],[9],[21],[31],[4],[30],[9],[9],[9],[22],[0],[9],[9],[9],[9],[9],[8],[11],[3],[7],[9],[14],[7],[9],[25],[16],[23],[9],[9],[10],[9],[9],[19],[24],[9],[12],[9],[9],[4],[6],[0],[0],[12],[8],[9],[9],[21],[9],[12],[1],[9],[9],[10],[10],[9],[9],[8],[9],[2],[20],[7],[9],[10],[15],[9],[11],[4],[4],[9],[10],[9],[9],[4],[26],[22],[9],[21],[9],[6],[25],[0],[15],[15],[9],[2],[21],[9],[9],[9],[4],[9],[20],[9],[7],[21],[21],[1],[9],[20],[24],[23],[9],[17],[9],[9],[9],[9],[24],[9],[12],[30],[9],[9],[23],[23],[23],[16],[18],[9],[9],[30],[31],[9],[9],[19],[9],[9],[14],[17],[19],[10],[13],[9],[13],[9],[18],[24],[4],[15],[8],[9],[9],[7],[20],[9],[9],[9],[8],[18],[9],[24],[0],[14],[5],[9],[7],[10],[9],[9],[9],[9],[9],[2],[4],[13],[9],[8],[9],[26],[25],[23],[9],[8],[9],[28],[12],[3],[16],[15],[9],[24],[18],[15],[9],[12],[9],[9],[9],[16],[9],[22],[6],[9],[20],[25],[19],[9],[18],[13],[15],[9],[28],[27],[9],[27],[9],[17],[14],[9],[9],[15],[7],[9],[0],[26],[9],[9],[9],[9],[30],[28],[9],[16],[9],[9],[9],[12],[9],[9],[8],[12],[9],[2],[9],[31],[20],[31],[7],[21],[5],[9],[9],[9],[18],[9],[9],[9],[15],[9],[9],[9],[13],[9],[16],[9],[10],[8],[9],[24],[9],[8],[12],[5],[9],[9],[9],[7],[19],[30],[9],[9],[9],[20],[7],[26],[30],[16],[9],[9],[9],[28],[7],[9],[9],[22],[9],[11],[29],[9],[9],[9],[9],[9],[9],[9],[9],[9],[9],[12],[22],[24],[9],[9],[9],[14],[2],[9],[5],[9],[13],[9],[26],[4],[9],[0],[22],[9],[16],[29],[9],[9],[9],[2],[17],[9],[26],[20],[9],[20],[9],[9],[20],[9],[9],[9],[9],[4],[25],[9],[18],[12],[15],[6],[9],[9],[9],[9],[16],[23],[1],[9],[9],[17],[9],[10],[12],[24],[4],[24],[9],[9],[12],[25],[9],[9],[9],[11],[9],[9],[3],[9],[11]],[[20],[0],[9],[9],[9],[1],[27],[9],[9],[9],[30],[22],[9],[10],[9],[9],[8],[1],[9],[25],[20],[2],[9],[12],[9],[28],[9],[12],[9],[10],[9],[9],[9],[17],[13],[9],[9],[20],[9],[9],[5],[3],[10],[17],[18],[17],[9],[27],[27],[3],[9],[9],[9],[7],[6],[3],[9],[31],[18],[31],[23],[9],[16],[20],[9],[6],[3],[9],[8],[13],[20],[9],[9],[11],[16],[9],[10],[1],[9],[3],[24],[14],[3],[9],[9],[20],[9],[5],[9],[9],[30],[13],[16],[9],[6],[9],[9],[8],[9],[25],[2],[9],[9],[9],[9],[2],[7],[18],[21],[9],[9],[9],[9],[18],[13],[22],[26],[21],[9],[9],[9],[8],[17],[7],[20],[9],[12],[10],[0],[17],[16],[16],[21],[20],[9],[30],[9],[9],[9],[22],[16],[14],[14],[5],[28],[9],[9],[3],[7],[14],[30],[9],[9],[7],[17],[9],[29],[5],[9],[9],[9],[3],[29],[9],[9],[31],[9],[9],[22],[9],[7],[8],[9],[19],[29],[3],[9],[1],[31],[9],[1],[9],[9],[31],[9],[30],[9],[25],[29],[3],[12],[9],[9],[4],[9],[9],[1],[10],[9],[9],[15],[9],[25],[13],[24],[9],[16],[11],[9],[9],[22],[0],[9],[31],[21],[9],[24],[19],[9],[16],[9],[28],[9],[9],[23],[30],[18],[9],[18],[0],[9],[9],[14],[17],[17],[10],[9],[12],[13],[9],[6],[9],[17],[24],[30],[9],[31],[21],[26],[9],[30],[9],[5],[11],[1],[9],[31],[27],[9],[16],[5],[13],[7],[19],[27],[9],[10],[9],[27],[9],[31],[23],[9],[25],[9],[20],[9],[27],[21],[4],[9],[15],[25],[9],[9],[15],[9],[9],[9],[20],[25],[18],[24],[9],[4],[10],[4],[15],[7],[9],[15],[22],[30],[9],[9],[9],[0],[9],[9],[29],[18],[12],[9],[16],[1],[5],[9],[26],[9],[9],[9],[13],[9],[9],[1],[17],[19],[9],[20],[1],[9],[27],[9],[28],[13],[12],[9],[11],[27],[2],[9],[1],[30],[9],[9],[30],[19],[9],[8],[9],[9],[9],[9],[9],[9],[3],[25],[2],[18],[9],[31],[11],[26],[20],[5],[14],[9],[6],[25],[3],[29],[31],[20],[22],[9],[27],[9],[3],[9],[4],[9],[14],[27],[21],[30],[10],[11],[1],[9],[15],[9],[31],[9],[15],[17],[21],[9],[9],[9],[9],[9],[9],[9],[11],[9],[9],[9],[24],[4],[11],[9],[9],[5],[9],[9],[19],[9],[9],[18],[13],[21],[9],[2],[17],[9],[0],[0],[21],[27],[15],[9],[9],[13],[9],[22],[9],[9],[14],[23],[9],[29],[7],[27],[24],[9],[8],[27],[8],[30],[25],[9],[9],[4],[9],[0],[26],[17],[9],[9],[9],[9],[17],[2],[9],[3],[3],[28],[12],[8],[2],[9],[0],[8],[9],[8],[12],[9],[9],[9],[31],[11],[9],[9],[9],[17],[9],[20],[9],[9],[9],[3],[9],[5],[9],[20],[5],[15],[15],[27],[27],[30],[26],[9],[9],[9],[3],[31],[10],[9],[9],[9],[9]],[[2],[3],[9],[6],[9],[9],[17],[9],[8],[9],[26],[23],[9],[16],[9],[9],[23],[9],[9],[12],[9],[9],[20],[9],[13],[15],[24],[3],[12],[10],[9],[7],[20],[24],[22],[9],[9],[3],[9],[5],[9],[9],[9],[4],[9],[9],[9],[9],[9],[7],[9],[3],[9],[16],[0],[23],[15],[9],[9],[9],[9],[15],[11],[9],[9],[15],[24],[9],[9],[9],[29],[9],[1],[29],[7],[13],[9],[9],[9],[9],[9],[5],[9],[9],[9],[9],[23],[9],[16],[9],[9],[27],[7],[15],[21],[1],[18],[2],[9],[25],[9],[6],[19],[29],[14],[9],[9],[27],[27],[14],[29],[9],[9],[0],[9],[9],[11],[10],[23],[7],[13],[10],[9],[9],[28],[9],[9],[8],[26],[9],[23],[9],[9],[20],[4],[3],[9],[9],[8],[16],[9],[9],[10],[3],[3],[14],[2],[31],[9],[4],[9],[9],[29],[9],[9],[18],[12],[2],[18],[24],[17],[9],[9],[31],[9],[18],[13],[9],[9],[9],[20],[4],[9],[24],[16],[31],[9],[9],[21],[9],[9],[9],[1],[9],[6],[9],[12],[6],[8],[9],[20],[28],[11],[9],[19],[9],[9],[7],[3],[22],[28],[9],[9],[9],[9],[9],[8],[9],[9],[16],[9],[9],[9],[9],[20],[27],[25],[5],[9],[17],[9],[4],[4],[16],[27],[18],[9],[9],[16],[12],[20],[9],[9],[21],[27],[8],[28],[14],[9],[9],[31],[9],[18],[9],[9],[30],[26],[9],[9],[9],[9],[2],[9],[9],[9],[11],[0],[8],[15],[9],[24],[9],[2],[3],[29],[9],[12],[9],[5],[30],[9],[9],[9],[9],[9],[9],[25],[16],[28],[14],[9],[16],[14],[9],[9],[9],[20],[1],[18],[15],[30],[9],[10],[9],[13],[1],[9],[5],[9],[30],[10],[12],[18],[5],[3],[9],[9],[9],[6],[16],[9],[9],[25],[3],[14],[29],[12],[18],[29],[10],[9],[10],[9],[19],[25],[9],[9],[20],[9],[9],[29],[9],[18],[5],[8],[9],[0],[25],[5],[9],[9],[25],[9],[8],[26],[9],[19],[9],[5],[17],[9],[9],[24],[20],[9],[25],[9],[12],[9],[15],[19],[31],[31],[21],[28],[0],[9],[25],[21],[9],[9],[5],[24],[30],[9],[7],[29],[12],[18],[9],[9],[26],[9],[2],[9],[30],[24],[7],[9],[13],[28],[9],[9],[19],[24],[11],[25],[9],[9],[19],[12],[17],[9],[9],[9],[30],[15],[27],[15],[28],[9],[31],[9],[9],[20],[9],[9],[9],[9],[9],[2],[4],[9],[9],[6],[9],[19],[17],[9],[9],[9],[9],[9],[1],[12],[9],[4],[9],[9],[31],[0],[10],[9],[19],[9],[11],[23],[9],[9],[13],[1],[0],[23],[9],[9],[9],[9],[9],[9],[9],[1],[9],[22],[30],[16],[0],[9],[14],[9],[9],[22],[14],[30],[17],[9],[14],[13],[9],[26],[17],[9],[9],[9],[15],[15],[24],[8],[7],[9],[9],[16],[23],[29],[27],[9],[15],[16],[27],[19],[9],[13],[6],[17],[15],[9],[28],[2],[27],[24],[15],[28],[20]],[[24],[9],[9],[14],[17],[15],[9],[13],[9],[28],[9],[31],[3],[7],[23],[9],[9],[9],[9],[18],[7],[3],[22],[25],[14],[29],[9],[9],[15],[18],[5],[0],[9],[19],[10],[10],[1],[9],[31],[9],[27],[26],[9],[24],[21],[9],[17],[29],[9],[2],[17],[9],[9],[26],[26],[25],[16],[18],[1],[9],[13],[21],[9],[22],[9],[22],[18],[12],[9],[8],[21],[9],[9],[14],[9],[9],[9],[22],[9],[29],[9],[9],[9],[7],[9],[9],[0],[9],[9],[9],[19],[18],[17],[6],[9],[25],[9],[14],[9],[19],[9],[9],[9],[0],[9],[21],[26],[9],[9],[28],[23],[9],[22],[5],[21],[11],[9],[9],[0],[9],[31],[9],[1],[7],[23],[9],[26],[9],[0],[9],[29],[9],[3],[9],[12],[9],[16],[9],[3],[9],[31],[9],[9],[17],[9],[9],[19],[7],[9],[21],[27],[9],[9],[30],[9],[9],[12],[5],[23],[14],[20],[30],[22],[9],[24],[11],[30],[9],[13],[0],[31],[4],[7],[2],[9],[17],[13],[22],[9],[11],[9],[22],[2],[9],[17],[29],[9],[25],[9],[9],[15],[9],[9],[28],[9],[1],[9],[9],[26],[10],[26],[9],[23],[2],[4],[9],[9],[11],[30],[28],[18],[9],[27],[30],[21],[6],[26],[12],[7],[22],[24],[15],[13],[9],[23],[22],[21],[7],[9],[25],[9],[31],[26],[9],[9],[9],[8],[9],[9],[9],[9],[3],[31],[15],[8],[9],[9],[9],[9],[9],[26],[9],[0],[10],[24],[9],[28],[9],[27],[5],[4],[23],[22],[14],[9],[9],[9],[6],[9],[9],[16],[26],[9],[9],[6],[28],[17],[17],[24],[28],[0],[9],[10],[22],[31],[9],[9],[9],[4],[9],[17],[4],[27],[7],[13],[26],[14],[9],[4],[9],[9],[9],[9],[24],[17],[9],[9],[3],[29],[9],[9],[9],[23],[9],[5],[27],[9],[9],[18],[9],[9],[31],[7],[20],[9],[9],[5],[15],[25],[9],[13],[9],[9],[24],[27],[9],[7],[20],[9],[23],[25],[12],[11],[12],[29],[9],[1],[21],[9],[9],[29],[17],[6],[2],[9],[2],[8],[9],[9],[14],[21],[9],[9],[30],[15],[28],[21],[18],[29],[27],[1],[18],[9],[9],[4],[31],[16],[10],[29],[9],[9],[16],[31],[9],[15],[3],[9],[9],[5],[8],[19],[12],[9],[21],[9],[22],[21],[19],[13],[6],[31],[9],[23],[9],[20],[19],[9],[9],[27],[1],[26],[9],[9],[18],[5],[9],[9],[9],[23],[31],[9],[9],[24],[9],[23],[21],[9],[9],[4],[9],[16],[7],[9],[9],[9],[21],[8],[13],[25],[13],[9],[1],[12],[18],[13],[8],[9],[15],[30],[9],[9],[10],[9],[19],[9],[18],[9],[5],[9],[8],[9],[17],[9],[2],[18],[26],[15],[23],[9],[9],[9],[9],[18],[9],[23],[24],[26],[9],[9],[18],[29],[18],[9],[16],[31],[9],[9],[31],[9],[18],[13],[9],[9],[16],[9],[11],[9],[21],[16],[22],[3],[9],[9],[16],[20],[3],[9],[30],[9],[9],[9],[9]],[[9],[9],[9],[18],[6],[9],[8],[30],[0],[9],[3],[9],[4],[4],[9],[14],[28],[14],[0],[22],[9],[13],[9],[27],[5],[31],[4],[9],[1],[9],[0],[23],[9],[9],[25],[21],[5],[9],[6],[13],[31],[30],[21],[11],[1],[9],[9],[17],[9],[9],[9],[9],[21],[31],[9],[9],[14],[7],[14],[9],[9],[18],[9],[31],[28],[22],[4],[5],[9],[9],[20],[14],[4],[9],[4],[29],[9],[12],[9],[9],[14],[9],[4],[9],[22],[9],[9],[9],[13],[28],[27],[26],[24],[9],[9],[27],[28],[9],[18],[9],[9],[9],[3],[9],[4],[8],[9],[9],[9],[9],[12],[17],[9],[5],[24],[26],[6],[9],[9],[9],[26],[4],[9],[9],[23],[9],[29],[18],[9],[2],[5],[9],[30],[3],[9],[4],[9],[9],[2],[16],[9],[14],[9],[14],[21],[9],[9],[9],[12],[22],[9],[9],[30],[31],[20],[9],[13],[9],[10],[15],[13],[6],[26],[9],[7],[9],[21],[9],[9],[23],[9],[9],[9],[9],[9],[9],[6],[29],[29],[9],[9],[21],[30],[9],[9],[9],[7],[5],[26],[9],[28],[9],[12],[8],[1],[9],[9],[13],[31],[10],[22],[9],[9],[18],[24],[9],[1],[11],[22],[9],[9],[9],[14],[9],[11],[26],[9],[28],[9],[9],[9],[28],[8],[9],[9],[9],[9],[25],[9],[0],[30],[9],[2],[9],[9],[0],[9],[9],[27],[9],[9],[24],[9],[28],[9],[20],[11],[9],[9],[10],[9],[9],[8],[9],[9],[9],[9],[9],[1],[3],[9],[9],[9],[9],[8],[9],[31],[28],[2],[18],[9],[9],[9],[22],[17],[27],[30],[5],[21],[17],[9],[1],[3],[9],[9],[1],[15],[23],[11],[8],[22],[9],[12],[9],[31],[20],[9],[29],[12],[9],[9],[3],[9],[31],[20],[22],[4],[9],[9],[16],[30],[9],[29],[25],[19],[9],[30],[2],[2],[9],[9],[9],[1],[8],[1],[29],[12],[9],[2],[10],[28],[9],[15],[9],[6],[26],[6],[1],[9],[9],[21],[2],[1],[9],[9],[9],[25],[9],[9],[2],[9],[31],[9],[29],[29],[10],[5],[16],[9],[9],[0],[19],[9],[9],[28],[9],[16],[18],[3],[9],[9],[17],[30],[9],[7],[7],[3],[6],[2],[9],[20],[9],[10],[7],[29],[9],[9],[30],[28],[20],[9],[1],[9],[9],[9],[30],[11],[2],[2],[20],[9],[10],[9],[31],[9],[13],[9],[9],[9],[9],[9],[28],[14],[17],[9],[7],[9],[6],[9],[19],[9],[9],[30],[11],[9],[15],[19],[11],[9],[23],[20],[2],[9],[18],[27],[9],[26],[27],[29],[6],[17],[9],[27],[4],[22],[9],[10],[21],[9],[9],[28],[9],[9],[0],[9],[26],[9],[9],[29],[13],[17],[9],[9],[9],[3],[10],[9],[9],[28],[23],[12],[25],[9],[21],[18],[9],[26],[5],[9],[1],[22],[9],[12],[9],[9],[9],[20],[9],[9],[4],[29],[9],[9],[9],[24],[9],[29],[9],[10],[9],[19],[9],[9],[20],[19],[9],[6],[9],[15],[9],[9],[9]],[[7],[1],[9],[9],[22],[9],[9],[12],[9],[14],[15],[9],[9],[9],[30],[22],[1],[1],[28],[9],[9],[9],[9],[18],[6],[9],[9],[11],[9],[9],[9],[1],[9],[9],[21],[16],[21],[3],[19],[15],[21],[9],[26],[9],[9],[17],[24],[27],[9],[20],[29],[9],[6],[9],[23],[22],[7],[1],[18],[27],[11],[9],[22],[9],[10],[9],[9],[9],[8],[31],[9],[10],[22],[2],[13],[29],[7],[9],[20],[9],[29],[7],[25],[28],[10],[9],[9],[9],[8],[13],[9],[9],[9],[9],[29],[3],[1],[1],[5],[22],[15],[4],[9],[3],[9],[0],[26],[25],[23],[16],[9],[0],[9],[18],[19],[13],[17],[15],[26],[6],[30],[23],[9],[16],[13],[30],[26],[25],[9],[11],[8],[28],[9],[9],[9],[20],[9],[29],[16],[9],[12],[27],[9],[10],[9],[9],[26],[9],[9],[27],[3],[12],[9],[9],[22],[0],[9],[9],[9],[21],[9],[9],[13],[11],[9],[18],[4],[9],[9],[9],[9],[9],[9],[9],[5],[9],[18],[9],[15],[9],[20],[16],[2],[5],[9],[16],[1],[14],[25],[30],[13],[9],[9],[9],[1],[10],[9],[14],[25],[5],[9],[20],[9],[9],[9],[9],[26],[9],[9],[9],[24],[13],[15],[2],[9],[5],[12],[9],[9],[6],[9],[9],[9],[1],[9],[3],[9],[9],[23],[27],[14],[24],[9],[21],[0],[9],[9],[20],[25],[29],[27],[6],[0],[29],[4],[9],[0],[19],[9],[21],[9],[19],[15],[29],[9],[8],[9],[11],[15],[9],[3],[9],[9],[5],[9],[7],[7],[12],[9],[9],[1],[24],[9],[6],[17],[9],[1],[16],[9],[28],[9],[9],[16],[22],[9],[18],[11],[9],[6],[5],[8],[24],[9],[9],[7],[9],[29],[25],[9],[9],[9],[9],[30],[2],[1],[23],[1],[25],[5],[25],[9],[9],[9],[9],[12],[21],[9],[13],[9],[9],[9],[26],[9],[9],[5],[2],[19],[9],[4],[20],[9],[15],[9],[7],[9],[30],[12],[31],[16],[24],[9],[30],[13],[9],[31],[20],[16],[3],[27],[9],[6],[9],[9],[7],[9],[7],[9],[25],[13],[9],[29],[9],[9],[0],[9],[7],[3],[31],[28],[4],[6],[16],[20],[9],[27],[9],[9],[9],[30],[21],[9],[21],[9],[27],[12],[1],[9],[8],[9],[9],[0],[28],[9],[29],[9],[11],[9],[11],[2],[1],[9],[9],[9],[18],[9],[9],[4],[9],[9],[4],[9],[10],[9],[9],[9],[9],[15],[30],[11],[29],[9],[9],[22],[7],[9],[18],[18],[9],[28],[1],[31],[23],[9],[9],[20],[22],[19],[6],[6],[4],[9],[9],[9],[4],[9],[9],[8],[9],[17],[9],[9],[10],[9],[13],[9],[10],[9],[15],[20],[1],[28],[9],[13],[22],[9],[9],[9],[22],[9],[9],[7],[3],[9],[20],[9],[30],[8],[8],[9],[9],[11],[9],[9],[26],[9],[9],[18],[9],[9],[25],[9],[9],[9],[2],[19],[5],[9],[9],[9],[9],[25],[9],[6],[9],[21],[11],[9],[9],[9],[9],[9],[20]],[[1],[22],[14],[28],[30],[27],[21],[9],[15],[9],[1],[9],[29],[26],[19],[22],[22],[17],[9],[9],[9],[22],[10],[9],[9],[19],[18],[21],[12],[30],[9],[8],[9],[19],[9],[9],[9],[9],[28],[4],[9],[18],[9],[9],[29],[4],[6],[9],[9],[11],[0],[9],[3],[3],[9],[9],[9],[20],[9],[7],[4],[9],[9],[30],[31],[30],[12],[9],[9],[16],[9],[9],[2],[16],[23],[9],[9],[9],[13],[20],[9],[21],[9],[23],[5],[9],[9],[29],[13],[26],[9],[9],[9],[24],[25],[17],[9],[13],[9],[9],[3],[1],[12],[31],[24],[9],[9],[24],[9],[9],[26],[11],[23],[13],[6],[5],[6],[29],[9],[9],[19],[0],[9],[25],[9],[9],[9],[9],[8],[13],[17],[9],[14],[13],[28],[9],[31],[28],[14],[9],[12],[13],[9],[0],[14],[0],[6],[29],[30],[9],[18],[9],[4],[14],[9],[9],[9],[10],[0],[10],[9],[29],[16],[25],[3],[9],[9],[9],[18],[28],[9],[31],[9],[8],[9],[1],[5],[9],[4],[9],[11],[9],[20],[9],[9],[9],[0],[8],[23],[9],[9],[2],[2],[11],[9],[31],[9],[4],[20],[9],[0],[17],[15],[7],[4],[23],[25],[5],[6],[29],[24],[5],[30],[22],[13],[6],[17],[25],[9],[9],[26],[26],[9],[3],[9],[9],[9],[9],[9],[22],[12],[18],[8],[27],[10],[27],[4],[28],[28],[9],[23],[9],[10],[16],[9],[9],[6],[9],[24],[3],[9],[9],[8],[9],[9],[13],[3],[9],[9],[13],[13],[24],[2],[9],[27],[9],[9],[9],[9],[9],[9],[9],[19],[22],[24],[6],[9],[9],[9],[2],[13],[18],[0],[9],[26],[25],[12],[30],[9],[9],[9],[9],[26],[23],[14],[11],[9],[9],[9],[25],[9],[9],[21],[9],[9],[5],[9],[30],[17],[9],[28],[9],[9],[21],[15],[26],[18],[9],[5],[14],[9],[9],[7],[15],[6],[9],[10],[11],[16],[18],[20],[9],[27],[9],[9],[9],[9],[20],[19],[9],[10],[25],[27],[3],[9],[15],[9],[9],[9],[25],[1],[9],[11],[17],[29],[30],[9],[9],[21],[16],[9],[9],[9],[9],[15],[13],[9],[18],[27],[21],[29],[9],[9],[17],[4],[2],[9],[9],[3],[2],[5],[9],[9],[8],[30],[9],[18],[9],[16],[13],[25],[30],[8],[11],[9],[30],[16],[28],[9],[21],[25],[5],[9],[25],[29],[18],[9],[31],[24],[9],[6],[9],[9],[9],[9],[9],[9],[24],[9],[9],[28],[12],[0],[9],[29],[5],[30],[12],[10],[19],[9],[9],[9],[27],[9],[30],[31],[1],[9],[9],[9],[3],[9],[9],[8],[25],[9],[9],[9],[5],[3],[23],[9],[9],[9],[24],[9],[2],[9],[4],[23],[12],[9],[9],[9],[3],[31],[21],[29],[9],[14],[16],[2],[8],[30],[0],[25],[24],[6],[4],[19],[4],[9],[9],[9],[26],[17],[17],[5],[9],[2],[9],[28],[16],[0],[9],[26],[25],[24],[9],[25],[8],[9],[5],[9],[12],[9],[9],[27],[27],[25],[9]],[[9],[9],[25],[27],[9],[8],[9],[17],[9],[9],[29],[9],[9],[9],[13],[9],[17],[9],[9],[9],[9],[25],[18],[9],[25],[24],[6],[9],[19],[21],[23],[31],[9],[22],[19],[9],[17],[9],[9],[1],[18],[9],[4],[25],[15],[9],[8],[9],[6],[9],[11],[15],[16],[9],[9],[9],[3],[9],[24],[9],[9],[21],[9],[23],[9],[24],[9],[11],[9],[6],[0],[9],[5],[20],[17],[27],[9],[21],[9],[28],[9],[22],[9],[9],[9],[9],[9],[22],[15],[22],[29],[11],[23],[5],[16],[2],[27],[9],[2],[27],[9],[9],[13],[9],[30],[9],[2],[9],[18],[17],[9],[6],[19],[9],[9],[9],[12],[9],[9],[11],[9],[9],[28],[28],[9],[9],[25],[19],[9],[9],[9],[21],[9],[9],[9],[2],[0],[9],[9],[3],[20],[9],[8],[9],[24],[9],[9],[0],[16],[30],[9],[7],[9],[9],[23],[6],[9],[9],[9],[29],[9],[25],[18],[1],[9],[22],[9],[20],[22],[21],[9],[9],[3],[9],[8],[5],[9],[9],[9],[9],[9],[3],[7],[9],[9],[9],[9],[30],[4],[30],[20],[9],[17],[16],[13],[15],[5],[30],[9],[21],[9],[2],[9],[1],[3],[12],[3],[9],[10],[1],[23],[10],[17],[6],[29],[22],[9],[2],[9],[10],[9],[1],[10],[12],[9],[9],[9],[8],[18],[9],[9],[9],[28],[29],[9],[16],[9],[5],[4],[10],[9],[19],[9],[10],[12],[10],[9],[9],[9],[16],[9],[29],[11],[26],[21],[9],[20],[23],[18],[9],[9],[9],[5],[9],[9],[9],[9],[9],[9],[9],[9],[25],[14],[8],[9],[9],[29],[9],[9],[26],[11],[3],[9],[9],[9],[9],[9],[1],[12],[9],[2],[24],[1],[3],[15],[9],[9],[9],[9],[11],[9],[9],[13],[12],[18],[3],[9],[18],[19],[12],[9],[1],[11],[9],[29],[9],[27],[13],[9],[9],[9],[20],[9],[2],[9],[19],[9],[9],[1],[9],[27],[0],[16],[28],[16],[28],[17],[19],[9],[9],[30],[5],[12],[18],[9],[17],[9],[24],[25],[9],[16],[6],[9],[9],[7],[19],[9],[15],[29],[24],[7],[16],[14],[9],[5],[9],[26],[15],[9],[9],[9],[9],[9],[9],[31],[7],[21],[24],[9],[9],[9],[10],[30],[9],[1],[22],[27],[1],[9],[9],[18],[12],[27],[2],[9],[0],[14],[20],[9],[1],[9],[21],[9],[13],[5],[9],[15],[9],[18],[10],[27],[9],[13],[12],[1],[23],[3],[23],[6],[28],[12],[9],[21],[9],[1],[9],[10],[25],[9],[9],[9],[9],[5],[21],[4],[9],[0],[26],[19],[9],[31],[7],[9],[14],[9],[25],[7],[24],[23],[16],[31],[4],[9],[7],[9],[29],[28],[9],[9],[2],[22],[14],[31],[9],[9],[17],[29],[9],[9],[18],[9],[2],[9],[9],[4],[9],[9],[9],[3],[3],[10],[17],[9],[7],[9],[27],[9],[1],[9],[21],[2],[9],[20],[9],[10],[6],[9],[0],[9],[30],[13],[20],[26],[0],[5],[9],[9],[18],[18],[9],[25],[3]],[[22],[14],[9],[9],[9],[10],[11],[22],[0],[9],[5],[7],[10],[24],[19],[9],[13],[9],[29],[6],[9],[3],[9],[25],[1],[12],[19],[22],[9],[14],[12],[12],[9],[9],[5],[9],[26],[9],[7],[16],[9],[9],[10],[9],[9],[20],[9],[9],[9],[26],[28],[13],[9],[9],[15],[9],[5],[27],[11],[9],[13],[13],[9],[22],[27],[17],[31],[0],[9],[24],[10],[28],[4],[9],[16],[26],[12],[29],[19],[9],[5],[10],[4],[11],[7],[9],[9],[18],[9],[9],[9],[15],[27],[29],[4],[9],[4],[24],[9],[0],[9],[9],[9],[9],[9],[9],[0],[9],[14],[9],[18],[9],[23],[1],[28],[9],[9],[2],[1],[9],[17],[9],[28],[3],[11],[10],[8],[21],[4],[14],[9],[28],[5],[9],[23],[9],[8],[13],[9],[9],[20],[9],[29],[9],[9],[9],[8],[9],[10],[9],[30],[22],[23],[9],[20],[22],[9],[26],[26],[9],[9],[14],[4],[15],[17],[9],[30],[9],[9],[17],[1],[22],[21],[22],[8],[17],[9],[20],[12],[11],[9],[16],[31],[26],[9],[22],[17],[9],[18],[9],[9],[9],[17],[26],[31],[24],[9],[3],[9],[16],[0],[27],[9],[12],[18],[30],[6],[9],[3],[27],[23],[29],[9],[9],[29],[8],[9],[9],[9],[9],[3],[22],[9],[9],[5],[11],[9],[8],[6],[9],[9],[9],[9],[9],[22],[29],[9],[9],[27],[9],[21],[13],[24],[9],[23],[6],[9],[9],[15],[9],[15],[11],[12],[9],[9],[26],[8],[9],[12],[5],[0],[11],[4],[9],[3],[9],[2],[20],[9],[9],[9],[9],[21],[19],[9],[9],[0],[29],[8],[30],[9],[9],[16],[24],[18],[20],[13],[4],[13],[8],[10],[4],[9],[9],[27],[9],[27],[8],[9],[9],[9],[9],[9],[19],[9],[0],[9],[19],[4],[2],[9],[9],[9],[12],[11],[15],[22],[12],[8],[30],[7],[9],[9],[9],[19],[26],[9],[1],[9],[17],[1],[19],[9],[9],[26],[29],[22],[15],[9],[9],[9],[31],[5],[17],[6],[30],[7],[9],[11],[19],[9],[9],[11],[9],[9],[9],[9],[24],[9],[3],[11],[28],[9],[30],[9],[9],[27],[9],[12],[17],[9],[30],[16],[10],[24],[9],[25],[9],[9],[16],[9],[24],[6],[9],[9],[25],[9],[9],[9],[9],[5],[9],[9],[9],[18],[14],[9],[19],[28],[6],[18],[7],[19],[0],[23],[9],[9],[9],[20],[22],[20],[9],[30],[25],[9],[21],[15],[13],[9],[26],[9],[17],[9],[9],[9],[1],[9],[16],[26],[10],[9],[8],[17],[9],[31],[9],[9],[9],[30],[30],[10],[9],[9],[9],[13],[9],[10],[3],[13],[9],[9],[9],[24],[9],[9],[18],[9],[9],[9],[0],[9],[14],[9],[3],[10],[23],[24],[9],[2],[13],[24],[9],[3],[9],[9],[9],[31],[9],[8],[22],[9],[9],[14],[9],[9],[9],[9],[21],[14],[31],[5],[9],[24],[28],[9],[6],[23],[11],[9],[9],[25],[9],[9],[9],[9],[9],[9],[13],[1],[9],[18],[9]],[[13],[8],[8],[6],[3],[3],[18],[8],[28],[27],[22],[9],[7],[25],[9],[9],[9],[5],[0],[30],[9],[30],[16],[9],[9],[26],[9],[14],[13],[9],[14],[9],[3],[9],[27],[19],[27],[9],[9],[9],[19],[0],[27],[9],[9],[9],[9],[15],[9],[7],[9],[9],[3],[29],[16],[29],[16],[9],[9],[9],[9],[9],[22],[21],[9],[6],[24],[9],[19],[26],[10],[6],[0],[9],[9],[9],[17],[17],[3],[20],[9],[9],[9],[29],[5],[9],[9],[9],[9],[27],[17],[18],[27],[9],[9],[12],[9],[9],[30],[14],[29],[27],[17],[23],[7],[31],[29],[9],[31],[23],[1],[22],[5],[14],[18],[21],[14],[0],[7],[24],[26],[9],[9],[9],[9],[3],[9],[17],[9],[9],[12],[9],[9],[7],[0],[9],[9],[14],[9],[17],[10],[24],[22],[9],[9],[9],[0],[12],[9],[9],[10],[8],[9],[9],[9],[24],[5],[1],[9],[9],[9],[9],[8],[3],[20],[7],[6],[18],[9],[9],[9],[4],[9],[9],[9],[27],[17],[0],[23],[13],[30],[31],[31],[30],[16],[25],[8],[9],[22],[10],[8],[9],[17],[9],[2],[21],[0],[9],[12],[30],[9],[9],[4],[9],[9],[3],[9],[29],[1],[9],[9],[9],[2],[1],[15],[9],[28],[9],[22],[9],[10],[17],[9],[4],[9],[9],[31],[9],[11],[25],[5],[9],[16],[25],[9],[9],[11],[9],[9],[9],[25],[9],[13],[16],[30],[11],[21],[9],[6],[9],[3],[9],[20],[28],[14],[13],[1],[17],[9],[9],[9],[27],[9],[13],[7],[28],[17],[17],[12],[9],[24],[2],[9],[9],[30],[21],[20],[7],[27],[21],[20],[9],[9],[12],[27],[13],[9],[24],[24],[12],[28],[9],[9],[14],[21],[9],[9],[19],[6],[9],[9],[9],[20],[2],[17],[8],[9],[9],[9],[19],[8],[9],[5],[25],[9],[9],[9],[9],[9],[9],[11],[9],[9],[23],[9],[9],[16],[13],[27],[12],[9],[9],[0],[9],[9],[4],[12],[2],[9],[4],[18],[28],[9],[9],[9],[9],[9],[9],[9],[9],[22],[2],[0],[16],[23],[31],[18],[9],[9],[11],[9],[24],[19],[4],[20],[14],[9],[9],[9],[22],[14],[19],[9],[9],[9],[26],[28],[3],[19],[25],[13],[9],[9],[19],[30],[12],[24],[2],[22],[17],[9],[4],[22],[8],[6],[7],[13],[9],[12],[9],[6],[9],[9],[26],[14],[9],[9],[28],[22],[4],[9],[9],[29],[9],[9],[9],[9],[9],[9],[25],[1],[9],[9],[19],[9],[17],[9],[23],[2],[29],[9],[28],[6],[9],[11],[1],[9],[9],[7],[10],[27],[30],[23],[28],[13],[10],[3],[23],[9],[9],[9],[9],[24],[9],[9],[9],[7],[9],[11],[9],[14],[14],[30],[1],[14],[19],[23],[31],[9],[19],[1],[7],[9],[2],[9],[3],[9],[9],[26],[0],[9],[11],[30],[9],[9],[0],[9],[11],[9],[9],[9],[19],[9],[28],[9],[2],[6],[9],[9],[24],[20],[9],[9],[2],[23],[8],[0],[7],[9],[17],[9],[31]],[[3],[9],[30],[9],[28],[9],[2],[22],[9],[9],[11],[9],[9],[26],[6],[29],[25],[13],[9],[5],[17],[2],[9],[27],[30],[7],[9],[9],[9],[26],[9],[9],[29],[20],[27],[9],[7],[17],[9],[20],[17],[24],[9],[9],[24],[9],[19],[28],[22],[2],[9],[30],[11],[30],[9],[27],[9],[22],[9],[9],[18],[12],[2],[27],[9],[1],[30],[9],[15],[14],[9],[25],[24],[20],[30],[3],[9],[9],[29],[9],[29],[0],[9],[9],[9],[2],[2],[23],[9],[2],[9],[9],[9],[0],[9],[9],[8],[18],[9],[9],[9],[26],[9],[9],[20],[28],[20],[9],[15],[9],[9],[3],[9],[15],[9],[9],[9],[30],[20],[16],[9],[10],[31],[0],[2],[11],[1],[9],[14],[19],[9],[8],[9],[16],[31],[11],[12],[9],[0],[31],[23],[28],[9],[9],[9],[14],[11],[9],[9],[5],[17],[5],[6],[18],[18],[9],[9],[9],[24],[9],[9],[9],[12],[15],[11],[9],[9],[21],[23],[9],[9],[9],[28],[9],[23],[12],[9],[22],[30],[24],[18],[9],[29],[28],[12],[13],[29],[26],[11],[10],[31],[9],[9],[8],[11],[15],[20],[4],[28],[9],[5],[0],[12],[6],[16],[9],[27],[9],[1],[9],[9],[27],[9],[25],[9],[10],[9],[15],[9],[9],[3],[14],[18],[27],[13],[9],[1],[9],[14],[9],[17],[9],[31],[9],[19],[9],[20],[16],[9],[9],[8],[3],[13],[18],[19],[26],[14],[20],[7],[1],[9],[23],[10],[4],[9],[9],[20],[16],[24],[23],[2],[9],[18],[28],[10],[4],[9],[0],[24],[14],[8],[19],[20],[26],[14],[9],[9],[27],[6],[0],[2],[22],[11],[19],[7],[4],[9],[24],[7],[9],[14],[31],[8],[15],[20],[14],[11],[0],[9],[9],[9],[9],[9],[9],[6],[9],[13],[19],[16],[12],[27],[30],[9],[22],[13],[9],[9],[31],[9],[19],[4],[12],[6],[9],[9],[9],[9],[28],[8],[9],[9],[9],[5],[1],[9],[10],[20],[5],[10],[12],[9],[9],[11],[9],[18],[2],[31],[28],[9],[9],[9],[27],[9],[4],[29],[24],[7],[8],[26],[24],[2],[21],[9],[24],[17],[31],[9],[5],[17],[9],[9],[9],[9],[28],[9],[26],[6],[9],[9],[0],[9],[9],[9],[23],[24],[1],[9],[9],[5],[10],[9],[17],[9],[23],[15],[7],[9],[14],[9],[13],[26],[10],[6],[30],[31],[20],[4],[0],[11],[27],[9],[23],[9],[20],[9],[9],[27],[8],[2],[19],[18],[14],[9],[21],[9],[23],[9],[30],[18],[9],[9],[9],[9],[9],[9],[9],[9],[9],[5],[26],[9],[6],[2],[2],[9],[21],[15],[9],[9],[9],[3],[9],[9],[9],[11],[9],[2],[19],[7],[16],[9],[7],[13],[27],[9],[18],[17],[9],[9],[0],[13],[12],[27],[9],[11],[9],[24],[18],[20],[9],[9],[31],[9],[26],[30],[11],[9],[31],[9],[31],[9],[11],[9],[10],[5],[30],[4],[15],[28],[30],[14],[11],[9],[7],[25],[9],[3],[9],[31],[9],[12],[2]],[[9],[9],[2],[15],[9],[5],[9],[9],[9],[19],[26],[2],[30],[14],[23],[9],[13],[9],[9],[3],[6],[30],[9],[9],[9],[21],[9],[18],[9],[11],[9],[12],[9],[9],[23],[9],[15],[9],[0],[9],[31],[9],[9],[20],[12],[9],[27],[12],[9],[29],[2],[9],[9],[9],[10],[9],[1],[6],[15],[9],[9],[28],[11],[9],[9],[9],[9],[29],[9],[3],[9],[28],[4],[30],[6],[30],[31],[31],[9],[9],[8],[9],[27],[9],[22],[22],[9],[13],[25],[9],[9],[9],[9],[9],[31],[2],[9],[18],[19],[9],[10],[26],[9],[17],[1],[31],[1],[14],[9],[22],[10],[12],[21],[23],[10],[28],[3],[22],[13],[9],[24],[29],[1],[9],[3],[21],[9],[16],[15],[18],[9],[9],[15],[26],[30],[9],[27],[9],[11],[9],[2],[3],[27],[17],[9],[9],[7],[7],[12],[9],[30],[26],[9],[17],[8],[9],[12],[9],[9],[9],[9],[9],[11],[16],[9],[9],[12],[9],[9],[11],[9],[29],[9],[9],[7],[9],[23],[14],[1],[4],[16],[9],[9],[6],[9],[29],[9],[9],[9],[3],[21],[30],[31],[9],[16],[15],[0],[15],[9],[14],[9],[22],[9],[7],[8],[9],[9],[9],[9],[9],[15],[19],[1],[9],[8],[9],[9],[18],[13],[9],[19],[9],[9],[16],[13],[9],[3],[31],[9],[1],[17],[9],[26],[14],[6],[13],[12],[9],[12],[9],[9],[11],[25],[9],[21],[13],[11],[2],[9],[9],[9],[1],[9],[9],[27],[9],[29],[9],[17],[9],[20],[9],[5],[29],[5],[31],[9],[9],[4],[12],[30],[9],[9],[9],[9],[20],[6],[16],[9],[9],[9],[3],[9],[14],[9],[16],[9],[9],[9],[9],[29],[9],[6],[21],[9],[9],[22],[30],[19],[27],[23],[9],[9],[5],[9],[9],[9],[22],[28],[9],[22],[9],[14],[9],[5],[13],[9],[9],[22],[9],[17],[29],[9],[9],[21],[20],[0],[8],[0],[18],[2],[9],[9],[13],[25],[9],[13],[9],[9],[22],[9],[9],[9],[20],[9],[9],[1],[18],[14],[7],[4],[17],[9],[9],[24],[9],[3],[9],[14],[12],[9],[12],[9],[6],[9],[9],[25],[22],[19],[12],[31],[9],[9],[9],[26],[1],[0],[14],[8],[9],[10],[9],[9],[17],[19],[1],[9],[9],[9],[23],[9],[14],[21],[8],[3],[20],[1],[10],[16],[9],[26],[14],[9],[23],[9],[9],[30],[23],[9],[17],[9],[15],[21],[9],[14],[15],[9],[15],[25],[9],[9],[10],[9],[9],[8],[9],[9],[23],[9],[21],[9],[9],[9],[21],[25],[13],[29],[12],[10],[7],[13],[9],[9],[9],[27],[5],[14],[8],[2],[9],[24],[9],[9],[7],[29],[20],[2],[18],[30],[9],[9],[31],[9],[9],[26],[9],[1],[30],[0],[9],[9],[12],[9],[9],[12],[29],[9],[8],[9],[0],[8],[9],[9],[6],[9],[15],[9],[9],[20],[24],[3],[12],[9],[9],[30],[9],[0],[18],[16],[28],[9],[13],[15],[20],[26],[9],[24],[3],[15],[17],[2],[2]],[[3],[9],[24],[9],[30],[22],[9],[24],[31],[18],[9],[9],[25],[1],[3],[9],[9],[22],[22],[9],[16],[23],[6],[9],[31],[9],[9],[3],[0],[9],[6],[19],[27],[9],[9],[2],[13],[9],[20],[14],[24],[9],[27],[9],[9],[22],[27],[13],[10],[9],[1],[14],[9],[10],[3],[1],[4],[22],[9],[9],[9],[9],[19],[0],[4],[25],[30],[24],[9],[3],[9],[15],[29],[9],[9],[8],[18],[9],[7],[5],[26],[27],[0],[9],[27],[11],[9],[12],[7],[9],[9],[4],[10],[27],[11],[23],[9],[9],[9],[10],[9],[29],[4],[9],[5],[9],[22],[4],[16],[10],[9],[21],[9],[8],[30],[9],[9],[31],[21],[9],[9],[20],[5],[24],[28],[9],[5],[28],[18],[9],[0],[3],[9],[9],[28],[3],[22],[9],[15],[29],[30],[9],[18],[1],[9],[9],[5],[30],[9],[9],[1],[18],[5],[30],[0],[9],[3],[9],[12],[24],[7],[9],[9],[25],[9],[20],[13],[5],[7],[9],[9],[28],[22],[10],[20],[9],[9],[17],[9],[14],[9],[25],[6],[9],[9],[20],[9],[21],[26],[20],[16],[9],[9],[18],[9],[24],[9],[17],[9],[9],[22],[7],[10],[9],[9],[30],[8],[9],[12],[9],[14],[15],[6],[25],[9],[25],[5],[9],[9],[30],[24],[18],[2],[2],[1],[20],[7],[19],[9],[4],[5],[9],[24],[2],[10],[0],[4],[9],[9],[3],[9],[8],[9],[14],[19],[31],[21],[26],[9],[23],[9],[12],[7],[18],[9],[25],[10],[9],[9],[20],[1],[15],[9],[9],[23],[30],[19],[2],[19],[9],[3],[29],[7],[9],[9],[6],[9],[9],[11],[29],[15],[9],[9],[9],[10],[4],[9],[1],[16],[2],[10],[9],[9],[9],[17],[9],[14],[9],[30],[1],[7],[29],[20],[9],[14],[9],[9],[0],[6],[30],[16],[2],[13],[20],[3],[5],[20],[7],[18],[9],[15],[4],[3],[10],[28],[6],[5],[23],[27],[18],[9],[8],[9],[9],[27],[9],[5],[9],[9],[9],[9],[31],[11],[0],[9],[10],[2],[9],[9],[28],[19],[13],[19],[15],[31],[9],[30],[14],[24],[25],[31],[9],[9],[10],[13],[20],[9],[9],[7],[14],[9],[9],[9],[9],[9],[21],[9],[27],[19],[17],[9],[9],[19],[20],[14],[9],[22],[2],[14],[11],[9],[9],[9],[9],[9],[3],[9],[6],[16],[5],[14],[7],[13],[30],[17],[15],[14],[9],[9],[9],[28],[9],[2],[2],[9],[9],[17],[22],[9],[30],[9],[11],[1],[4],[31],[22],[22],[9],[9],[2],[1],[18],[9],[9],[14],[4],[28],[18],[0],[9],[5],[31],[4],[9],[31],[9],[1],[26],[9],[9],[9],[9],[9],[25],[9],[9],[16],[9],[7],[9],[2],[9],[23],[9],[9],[9],[26],[9],[16],[26],[17],[9],[9],[31],[9],[15],[18],[23],[6],[19],[13],[8],[17],[28],[9],[9],[11],[9],[9],[9],[9],[9],[9],[30],[29],[17],[23],[20],[31],[9],[9],[25],[27],[9],[0],[4],[9],[1],[5],[31],[17],[17]],[[3],[9],[9],[9],[11],[1],[22],[27],[4],[20],[30],[21],[8],[9],[11],[11],[2],[31],[9],[9],[9],[6],[2],[3],[27],[5],[9],[3],[31],[9],[9],[26],[9],[2],[9],[2],[2],[9],[2],[10],[7],[9],[16],[28],[9],[2],[18],[20],[9],[9],[12],[9],[15],[30],[9],[9],[9],[12],[7],[2],[10],[2],[26],[9],[4],[27],[1],[5],[9],[20],[1],[25],[9],[9],[9],[9],[24],[9],[9],[10],[18],[9],[9],[9],[9],[9],[9],[9],[9],[9],[2],[9],[9],[27],[5],[9],[12],[3],[2],[20],[9],[21],[3],[8],[9],[4],[0],[31],[20],[9],[14],[9],[1],[14],[9],[9],[9],[16],[15],[9],[8],[9],[9],[21],[29],[21],[14],[9],[9],[14],[3],[15],[28],[13],[0],[31],[13],[23],[9],[9],[22],[16],[9],[18],[7],[31],[27],[5],[5],[9],[9],[23],[9],[11],[9],[9],[9],[10],[19],[9],[8],[9],[9],[3],[9],[14],[9],[24],[9],[15],[9],[29],[9],[9],[7],[5],[9],[2],[9],[7],[19],[9],[0],[9],[9],[27],[1],[9],[9],[29],[9],[9],[23],[10],[24],[6],[5],[9],[1],[31],[15],[3],[16],[9],[22],[7],[6],[9],[17],[24],[9],[14],[10],[9],[8],[30],[22],[17],[9],[9],[9],[9],[9],[9],[9],[9],[29],[7],[4],[9],[25],[26],[9],[22],[9],[9],[1],[9],[27],[13],[1],[27],[9],[9],[6],[31],[9],[31],[9],[9],[27],[9],[9],[18],[9],[2],[0],[9],[28],[9],[9],[23],[9],[0],[29],[9],[9],[9],[31],[24],[0],[27],[28],[18],[25],[25],[5],[9],[0],[9],[17],[20],[2],[28],[31],[31],[10],[2],[7],[9],[22],[17],[5],[8],[25],[16],[9],[9],[19],[1],[23],[9],[9],[9],[9],[18],[9],[29],[23],[14],[21],[7],[9],[9],[9],[31],[9],[21],[23],[9],[17],[9],[9],[26],[3],[27],[9],[6],[11],[9],[13],[1],[9],[9],[9],[13],[9],[10],[9],[2],[21],[29],[6],[0],[25],[18],[9],[23],[9],[30],[9],[9],[9],[9],[11],[19],[19],[9],[9],[22],[5],[30],[14],[9],[9],[5],[9],[9],[12],[15],[9],[27],[9],[9],[9],[9],[11],[24],[4],[9],[7],[9],[9],[23],[5],[30],[9],[16],[9],[30],[9],[15],[14],[19],[9],[9],[8],[9],[9],[9],[9],[6],[9],[0],[9],[28],[30],[9],[9],[9],[5],[9],[9],[9],[28],[9],[9],[9],[31],[9],[10],[11],[9],[9],[9],[8],[1],[2],[9],[9],[9],[3],[9],[27],[2],[26],[9],[9],[9],[9],[9],[9],[9],[10],[9],[9],[9],[5],[17],[16],[9],[0],[27],[26],[22],[15],[9],[1],[0],[21],[9],[9],[6],[2],[5],[0],[21],[8],[14],[26],[27],[14],[9],[9],[18],[20],[9],[18],[6],[9],[31],[9],[9],[21],[22],[31],[27],[9],[16],[10],[7],[7],[21],[1],[9],[21],[21],[11],[9],[9],[10],[9],[8],[9],[30],[12],[25],[2],[24],[9],[9],[9]],[[9],[24],[9],[9],[9],[26],[9],[9],[9],[9],[2],[16],[18],[9],[9],[9],[13],[0],[21],[8],[26],[15],[27],[9],[23],[27],[9],[9],[9],[31],[4],[9],[9],[21],[17],[9],[21],[13],[0],[9],[9],[9],[15],[5],[15],[27],[9],[9],[9],[9],[12],[9],[9],[31],[9],[11],[9],[0],[10],[3],[9],[9],[21],[9],[9],[2],[1],[8],[9],[9],[26],[15],[9],[9],[13],[26],[7],[9],[2],[13],[1],[5],[8],[9],[20],[9],[18],[9],[30],[23],[21],[16],[2],[27],[9],[3],[9],[5],[9],[23],[29],[15],[24],[9],[10],[9],[9],[9],[7],[26],[3],[28],[9],[9],[30],[15],[9],[16],[26],[1],[27],[17],[17],[20],[6],[23],[7],[27],[4],[24],[9],[9],[20],[31],[9],[9],[10],[20],[6],[9],[8],[9],[9],[9],[9],[10],[9],[8],[25],[9],[3],[9],[27],[18],[2],[9],[9],[9],[9],[9],[8],[7],[8],[26],[12],[27],[9],[9],[28],[9],[13],[4],[9],[9],[17],[12],[8],[3],[27],[9],[17],[29],[20],[9],[9],[9],[20],[9],[21],[8],[9],[0],[26],[31],[31],[1],[0],[28],[8],[15],[9],[9],[9],[9],[9],[9],[14],[9],[9],[10],[18],[9],[9],[5],[4],[9],[11],[24],[10],[18],[0],[10],[9],[20],[30],[9],[9],[0],[9],[9],[9],[9],[9],[17],[9],[9],[9],[9],[31],[9],[25],[22],[9],[22],[9],[0],[1],[9],[0],[0],[9],[9],[11],[20],[11],[7],[9],[9],[6],[9],[9],[6],[13],[13],[11],[25],[9],[4],[9],[11],[16],[0],[10],[13],[5],[9],[19],[27],[27],[2],[9],[9],[20],[25],[16],[9],[27],[4],[9],[9],[15],[18],[9],[9],[30],[9],[3],[29],[22],[0],[9],[24],[9],[1],[27],[9],[23],[25],[11],[5],[5],[3],[9],[28],[9],[9],[9],[10],[9],[9],[31],[9],[2],[9],[9],[9],[2],[10],[2],[3],[9],[18],[13],[9],[9],[2],[9],[14],[21],[6],[19],[9],[2],[9],[4],[18],[13],[9],[20],[9],[9],[27],[9],[9],[23],[26],[22],[5],[4],[9],[28],[20],[9],[11],[30],[9],[9],[9],[30],[9],[9],[9],[26],[20],[9],[9],[9],[10],[9],[9],[28],[9],[13],[7],[24],[9],[21],[7],[9],[17],[24],[9],[1],[9],[14],[9],[1],[12],[25],[18],[9],[11],[4],[9],[4],[9],[9],[13],[10],[9],[9],[12],[15],[9],[9],[29],[9],[9],[9],[1],[31],[30],[1],[9],[12],[11],[29],[9],[9],[17],[7],[7],[9],[15],[11],[25],[31],[9],[25],[9],[24],[11],[9],[7],[3],[9],[8],[9],[20],[15],[14],[25],[4],[10],[20],[15],[9],[9],[9],[18],[6],[22],[28],[24],[6],[9],[22],[8],[12],[18],[9],[1],[9],[30],[29],[9],[9],[9],[24],[17],[9],[9],[14],[1],[9],[9],[2],[7],[9],[20],[29],[9],[1],[9],[12],[9],[11],[19],[9],[9],[9],[23],[30],[1],[9],[5],[21],[9],[9],[2],[12],[9]],[[23],[9],[9],[9],[25],[12],[16],[9],[9],[8],[3],[9],[21],[2],[21],[27],[9],[21],[9],[16],[26],[9],[23],[21],[1],[9],[1],[9],[5],[26],[9],[13],[9],[9],[9],[17],[9],[29],[9],[9],[25],[19],[9],[9],[3],[9],[14],[16],[9],[12],[18],[11],[9],[18],[3],[9],[9],[9],[23],[9],[26],[15],[9],[24],[9],[15],[9],[24],[1],[25],[9],[9],[2],[9],[9],[5],[9],[9],[9],[19],[10],[9],[24],[18],[15],[9],[25],[4],[8],[9],[9],[9],[21],[27],[0],[31],[9],[17],[3],[18],[9],[9],[9],[28],[9],[29],[27],[1],[9],[17],[0],[23],[31],[9],[9],[23],[9],[4],[9],[9],[5],[25],[9],[21],[9],[9],[31],[23],[9],[16],[9],[16],[9],[9],[16],[31],[24],[25],[21],[7],[21],[9],[9],[9],[12],[10],[4],[9],[18],[16],[23],[9],[15],[9],[12],[31],[9],[23],[16],[22],[9],[9],[23],[9],[26],[15],[9],[19],[9],[9],[9],[18],[14],[9],[31],[24],[7],[14],[6],[9],[1],[20],[9],[22],[9],[6],[18],[19],[3],[25],[9],[30],[9],[9],[1],[28],[9],[26],[9],[21],[0],[2],[29],[5],[9],[13],[6],[6],[9],[9],[24],[9],[9],[0],[6],[17],[22],[9],[8],[21],[15],[27],[26],[20],[9],[29],[9],[9],[6],[23],[9],[16],[9],[9],[13],[30],[9],[7],[9],[31],[15],[9],[3],[23],[3],[4],[9],[13],[9],[19],[26],[9],[29],[9],[23],[9],[9],[23],[5],[9],[10],[13],[9],[17],[9],[4],[9],[17],[9],[25],[9],[9],[17],[1],[23],[6],[22],[19],[9],[1],[17],[9],[23],[9],[29],[7],[9],[9],[19],[25],[9],[9],[1],[16],[9],[31],[9],[10],[11],[21],[9],[29],[9],[8],[28],[26],[18],[9],[9],[7],[25],[9],[15],[9],[9],[8],[12],[9],[9],[2],[9],[9],[9],[9],[25],[2],[9],[11],[12],[23],[8],[9],[9],[9],[9],[0],[30],[9],[27],[10],[18],[31],[5],[20],[9],[31],[9],[0],[2],[18],[9],[9],[9],[30],[11],[10],[11],[25],[9],[24],[3],[21],[11],[9],[29],[9],[9],[19],[22],[4],[9],[2],[29],[20],[5],[15],[9],[17],[10],[9],[26],[20],[27],[23],[9],[9],[17],[0],[7],[9],[9],[19],[20],[6],[9],[12],[9],[9],[4],[18],[9],[7],[4],[0],[10],[5],[9],[9],[2],[23],[12],[9],[9],[8],[9],[29],[9],[9],[19],[14],[12],[17],[25],[24],[7],[25],[9],[9],[9],[9],[5],[7],[10],[3],[26],[26],[29],[9],[9],[9],[11],[9],[9],[15],[9],[30],[7],[9],[9],[17],[17],[9],[27],[9],[16],[9],[9],[9],[17],[10],[9],[9],[9],[9],[2],[9],[27],[4],[29],[9],[2],[31],[23],[9],[9],[19],[9],[0],[9],[9],[2],[11],[1],[1],[9],[0],[9],[1],[6],[16],[25],[9],[9],[28],[9],[9],[9],[31],[9],[9],[27],[9],[7],[28],[9],[9],[11],[9],[15],[19],[28],[9]],[[26],[5],[15],[4],[9],[25],[9],[8],[9],[27],[23],[0],[9],[9],[15],[9],[9],[9],[2],[9],[9],[9],[9],[9],[9],[7],[2],[9],[9],[20],[9],[9],[9],[9],[9],[9],[10],[11],[9],[9],[25],[6],[9],[9],[23],[9],[24],[9],[9],[29],[28],[20],[9],[8],[11],[8],[28],[9],[28],[23],[15],[1],[9],[14],[9],[8],[3],[7],[23],[29],[9],[13],[9],[2],[18],[29],[9],[19],[9],[9],[9],[20],[2],[15],[9],[15],[9],[9],[31],[9],[6],[20],[9],[26],[18],[9],[9],[14],[13],[31],[9],[8],[9],[16],[9],[9],[26],[7],[18],[9],[9],[9],[13],[29],[23],[9],[1],[26],[27],[31],[11],[9],[8],[7],[9],[29],[9],[9],[20],[4],[20],[22],[1],[2],[31],[9],[9],[24],[25],[9],[9],[14],[9],[11],[9],[30],[9],[9],[20],[26],[9],[9],[9],[4],[27],[1],[9],[9],[2],[24],[18],[13],[1],[9],[9],[21],[3],[24],[9],[14],[26],[12],[20],[28],[6],[1],[6],[10],[9],[16],[28],[21],[9],[9],[9],[9],[9],[9],[9],[9],[22],[9],[23],[9],[25],[19],[9],[4],[19],[3],[1],[9],[29],[9],[9],[26],[27],[13],[26],[19],[9],[16],[9],[27],[1],[9],[27],[4],[19],[9],[11],[21],[9],[9],[9],[9],[1],[20],[21],[5],[2],[9],[9],[12],[10],[1],[9],[2],[9],[2],[2],[21],[9],[29],[4],[22],[26],[7],[19],[9],[9],[9],[9],[20],[9],[11],[5],[9],[29],[9],[12],[9],[26],[9],[9],[24],[9],[7],[20],[3],[15],[7],[30],[9],[19],[9],[9],[29],[21],[9],[9],[9],[10],[9],[8],[9],[6],[12],[31],[9],[13],[6],[11],[29],[13],[1],[8],[6],[23],[9],[1],[23],[4],[15],[12],[29],[9],[4],[9],[2],[9],[9],[9],[9],[17],[9],[28],[8],[9],[26],[9],[9],[1],[9],[0],[24],[9],[2],[6],[10],[15],[9],[28],[25],[19],[9],[9],[2],[9],[9],[9],[0],[2],[8],[9],[9],[19],[9],[30],[30],[9],[24],[19],[9],[1],[9],[9],[26],[9],[17],[1],[9],[9],[9],[9],[26],[28],[9],[9],[16],[9],[18],[31],[5],[25],[13],[13],[19],[9],[14],[9],[12],[9],[24],[25],[6],[8],[3],[9],[3],[16],[21],[8],[9],[7],[27],[9],[9],[27],[16],[8],[3],[1],[9],[9],[20],[9],[22],[13],[9],[9],[16],[18],[23],[9],[2],[8],[9],[26],[9],[10],[8],[9],[0],[13],[9],[24],[14],[22],[9],[9],[13],[31],[9],[9],[9],[29],[17],[9],[22],[17],[20],[2],[9],[16],[9],[14],[7],[18],[4],[9],[9],[24],[2],[1],[22],[12],[27],[22],[9],[9],[6],[21],[9],[1],[1],[9],[7],[4],[9],[9],[1],[11],[0],[9],[22],[9],[9],[9],[9],[9],[9],[11],[17],[9],[25],[9],[16],[9],[9],[23],[15],[24],[2],[9],[9],[5],[9],[9],[6],[9],[5],[9],[19],[31],[9],[9],[19],[9],[14],[4],[9]],[[9],[8],[26],[17],[5],[31],[13],[0],[9],[11],[8],[9],[10],[1],[9],[9],[30],[9],[6],[30],[9],[15],[9],[9],[9],[9],[23],[31],[24],[2],[9],[24],[28],[23],[11],[23],[9],[14],[27],[9],[26],[22],[9],[31],[31],[9],[30],[8],[14],[13],[9],[9],[28],[24],[9],[25],[11],[9],[29],[9],[18],[20],[21],[12],[9],[12],[23],[7],[11],[1],[25],[9],[4],[11],[9],[3],[9],[9],[9],[8],[9],[23],[9],[9],[29],[9],[9],[9],[0],[9],[18],[4],[1],[7],[15],[30],[10],[30],[9],[10],[9],[5],[9],[9],[3],[14],[18],[23],[9],[28],[19],[16],[29],[8],[26],[9],[9],[9],[24],[29],[13],[27],[1],[26],[9],[9],[24],[8],[9],[9],[1],[9],[9],[9],[17],[9],[2],[0],[12],[0],[30],[30],[9],[9],[2],[27],[18],[9],[9],[2],[0],[9],[14],[9],[18],[11],[9],[14],[2],[7],[18],[18],[9],[3],[8],[10],[5],[9],[9],[24],[29],[11],[9],[23],[9],[6],[9],[21],[9],[9],[31],[9],[23],[9],[6],[22],[9],[9],[30],[6],[9],[0],[29],[28],[9],[12],[8],[11],[9],[27],[9],[9],[16],[9],[9],[3],[9],[9],[17],[9],[1],[2],[10],[16],[9],[10],[9],[20],[29],[24],[9],[11],[5],[21],[29],[9],[9],[9],[24],[9],[9],[2],[30],[9],[9],[8],[26],[2],[15],[9],[18],[31],[9],[9],[9],[25],[9],[9],[9],[19],[16],[9],[11],[4],[9],[8],[28],[19],[12],[24],[9],[18],[16],[9],[9],[10],[25],[15],[16],[0],[9],[9],[9],[28],[20],[27],[31],[8],[9],[21],[14],[18],[9],[5],[8],[9],[14],[9],[10],[9],[9],[9],[13],[9],[9],[4],[9],[9],[9],[26],[9],[0],[9],[9],[29],[9],[9],[18],[9],[25],[9],[5],[30],[29],[9],[9],[9],[15],[19],[19],[9],[9],[9],[27],[7],[1],[9],[8],[9],[28],[9],[11],[9],[9],[10],[6],[9],[9],[17],[9],[9],[29],[25],[9],[2],[9],[4],[29],[22],[6],[27],[9],[9],[9],[10],[9],[9],[17],[9],[0],[13],[9],[5],[8],[0],[12],[24],[19],[2],[9],[28],[23],[9],[28],[23],[9],[9],[9],[9],[9],[30],[28],[9],[9],[7],[30],[2],[18],[27],[4],[27],[16],[29],[11],[9],[1],[23],[30],[12],[8],[9],[9],[28],[9],[15],[9],[9],[9],[20],[9],[30],[9],[5],[9],[7],[9],[20],[22],[9],[27],[9],[9],[18],[9],[24],[26],[9],[9],[12],[9],[4],[21],[9],[6],[9],[9],[9],[9],[3],[9],[9],[29],[23],[9],[9],[27],[9],[3],[7],[12],[9],[9],[9],[9],[9],[9],[6],[28],[9],[4],[9],[20],[29],[1],[6],[27],[29],[31],[9],[5],[9],[11],[13],[9],[9],[6],[9],[28],[22],[22],[8],[16],[9],[9],[10],[9],[9],[10],[9],[9],[21],[13],[9],[31],[9],[26],[9],[27],[9],[28],[9],[7],[9],[9],[9],[21],[0],[9],[15],[9],[9],[1]]]
CAP = 387
YW = 387
def setup_inputs(rng):
    return {"x": rng.standard_normal((N, 128, T), dtype=np.float32)}
def reference(x):
    y = np.full((N, 128, YW), np.nan, x.dtype)
    fill = [0] * N
    for r in range(N):
        for t in range(T):
            for e in ROUTE[r][t]:
                if fill[e] < CAP:
                    y[e][:, fill[e]] = x[r][:, t]
                fill[e] += 1
    return {"y": y}

@@ -1,0 +1,129 @@
+SCRATCH = {
+    "xs": ("sbuf", [128, 512], "float32"),
+    "pk": ("sbuf", [128, 512], "float32"),
+    "rel": ("sbuf", [128, 512], "float32"),
+    "land": ("sbuf", [128, 387], "float32"),
+}
+SEMAPHORES = ["loaded", "packed", "sent", "arrived", "relin", "stored"]
+
+
+def make_plan(T):
+    route = T.tables["ROUTE"]
+    cap = T.tables["CAP"]
+    n = len(route)
+    fill = [0] * n
+    kept = [[[] for _ in range(n)] for _ in range(n)]
+    off = [[0] * n for _ in range(n)]
+    for r in range(n):
+        for t in range(len(route[r])):
+            for e in route[r][t]:
+                if fill[e] < cap:
+                    if not kept[r][e]:
+                        off[r][e] = fill[e]
+                    kept[r][e].append(t)
+                fill[e] += 1
+    cnt = [min(f, cap) for f in fill]
+    return n, kept, off, cnt
+
+
+def runs_of(tokens):
+    out = []
+    for t in tokens:
+        if out and out[-1][0] + out[-1][1] == t:
+            out[-1][1] += 1
+        else:
+            out.append([t, 1])
+    return out
+
+
+def relay_of(core):
+    return (core // 8) * 8 + 6
+
+
+def bits(m):
+    return bin(m).count("1")
+
+
+def layout(r, T, topo, n, kept):
+    c = T.cores[r]
+    direct = [e for e in range(n) if e != r and kept[r][e] and topo.may_write(c, T.cores[e])]
+    relay = [e for e in range(n) if e != r and kept[r][e] and not topo.may_write(c, T.cores[e])]
+    pos = {}
+    o = 0
+    for e in direct + relay:
+        pos[e] = o
+        o += len(kept[r][e])
+    return direct, relay, pos, o
+
+
+def rank_program(g, core, T, topo):
+    n, kept, off, cnt = make_plan(T)
+    rank = T.rank_of(core)
+    S = T.sem
+
+    def send(src_ap, e, r):
+        dst = T.cores[e]
+        rid, pid, _se = topo.addr(dst)
+        m = topo.mask(core, dst)
+        w = len(kept[r][e])
+        g.remote_dma(T.land[:, off[r][e]:off[r][e] + w], src_ap, S.arrived, S.sent, pid, rid, m)
+        return bits(m)
+
+    if rank is None:
+        if core % 8 != 6:
+            return
+        src = (core // 8) * 8 + 1
+        r = T.rank_of(src)
+        if r is None:
+            return
+        direct, relay, pos, tot = layout(r, T, topo, n, kept)
+        if not relay:
+            return
+        g.wait_ge(S.relin, 16)
+        base = pos[relay[0]]
+        s = 0
+        for e in relay:
+            w = len(kept[r][e])
+            s += send(T.rel[:, pos[e] - base:pos[e] - base + w], e, r)
+        g.wait_ge(S.sent, s)
+        return
+
+    r = rank
+    direct, relay, pos, tot = layout(r, T, topo, n, kept)
+    g.sync.dma_start(T.xs[:], T.x[:]).then_inc(S.loaded, 16)
+    g.sync.wait_ge(S.loaded, 16)
+    g.scalar.wait_ge(S.loaded, 16)
+    qs = [g.sync, g.scalar]
+    k = 0
+    for e in direct + relay + [r]:
+        o = off[r][r] if e == r else pos[e]
+        buf = T.land if e == r else T.pk
+        for t, w in runs_of(kept[r][e]):
+            qs[k % 2].dma_start(buf[:, o:o + w], T.xs[:, t:t + w]).then_inc(S.packed, 16)
+            o += w
+            k += 1
+    g.wait_ge(S.packed, 16 * k)
+    s = 0
+    if relay:
+        base = pos[relay[0]]
+        rc = relay_of(core)
+        rid, pid, _se = topo.addr(rc)
+        g.remote_dma(T.rel[:, 0:tot - base], T.pk[:, base:tot], S.relin, S.sent, pid, rid, 0xFFFF)
+        s += 16
+    for e in direct:
+        w = len(kept[r][e])
+        s += send(T.pk[:, pos[e]:pos[e] + w], e, r)
+    a = 0
+    for q in range(n):
+        if q != r and kept[q][r]:
+            sc = T.cores[q]
+            if not topo.may_write(sc, core):
+                sc = relay_of(sc)
+            a += bits(topo.mask(sc, core))
+    g.sync.wait_ge(S.packed, 16 * k)
+    g.sync.wait_ge(S.arrived, a)
+    g.sync.dma_start(T.y[:, 0:cnt[r]], T.land[:, 0:cnt[r]]).then_inc(S.stored, 16)
+    g.sync.wait_ge(S.stored, 16)
+    g.wait_ge(S.sent, s)
+    g.wait_ge(S.arrived, a)
+    g.wait_ge(S.stored, 16)

@@ -1,15 +1,69 @@
+from concourse.bass import DstId, RemoteDMATransfer
+
+STEPPED = False
+NPK = 16
+
 SCRATCH = {
-    "xs": ("sbuf", [128, 512], "float32"),
-    "pk": ("sbuf", [128, 512], "float32"),
-    "rel": ("sbuf", [128, 512], "float32"),
-    "land": ("sbuf", [128, 387], "float32"),
+    "xs": ("sbuf", [128, 512, 1], "float32"),
+    "pk": ("sbuf", [128, 512, 1], "float32"),
+    "land": ("sbuf", [128, 387, 1], "float32"),
 }
-SEMAPHORES = ["loaded", "packed", "sent", "arrived", "relin", "stored"]
+SEMAPHORES = ["loaded", "xin", "own", "sent", "arrived", "stored"] + ["pk%d" % i for i in range(NPK)]
+
+TEAM = {1: (1, 3, 5, 7), 2: (2, 0, 4, 6)}
+BIG, PIECE = 24, 10
+POWER = 8
+CACHE = {}
 
 
-def make_plan(T):
-    route = T.tables["ROUTE"]
-    cap = T.tables["CAP"]
+def runs_of(tokens):
+    out = []
+    for t in tokens:
+        if out and out[-1][0] + out[-1][1] == t:
+            out[-1][1] += 1
+        else:
+            out.append([t, 1])
+    return out
+
+
+def segments(runs):
+    out = []
+    i = 0
+    while i < len(runs):
+        if runs[i][1] > 1 or not STEPPED:
+            out.append((runs[i][0], 1, runs[i][1]))
+            i += 1
+            continue
+        j = i
+        while j < len(runs) and runs[j][1] == 1:
+            j += 1
+        ts = [q[0] for q in runs[i:j]]
+        m = len(ts)
+        best = [0] + [m + 1] * m
+        prev = [0] * (m + 1)
+        for a in range(m):
+            b = a + 1
+            while True:
+                if best[a] + 1 < best[b]:
+                    best[b] = best[a] + 1
+                    prev[b] = a
+                if b >= m or (b - a >= 2 and ts[b] - ts[b - 1] != ts[a + 1] - ts[a]):
+                    break
+                b += 1
+        cuts = [m]
+        while cuts[-1] > 0:
+            cuts.append(prev[cuts[-1]])
+        cuts.reverse()
+        for a, b in zip(cuts[:-1], cuts[1:]):
+            out.append((ts[a], ts[a + 1] - ts[a] if b - a > 1 else 1, b - a))
+        i = j
+    return out
+
+
+def make_plan(T, topo):
+    if "plan" in CACHE:
+        return CACHE["plan"]
+    route, cap, cores = T.tables["ROUTE"], T.tables["CAP"], T.cores
     n = len(route)
     fill = [0] * n
     kept = [[[] for _ in range(n)] for _ in range(n)]
@@ -23,107 +77,155 @@ def make_plan(T):
                     kept[r][e].append(t)
                 fill[e] += 1
     cnt = [min(f, cap) for f in fill]
-    return n, kept, off, cnt
 
+    team = [[cores[r] // 8 * 8 + k for k in TEAM[cores[r] % 8]] for r in range(n)]
+    leader = {}
+    for r in range(n):
+        for s in team[r]:
+            leader[s] = r
 
-def runs_of(tokens):
-    out = []
-    for t in tokens:
-        if out and out[-1][0] + out[-1][1] == t:
-            out[-1][1] += 1
+    pieces = []
+    for r in range(n):
+        for e in range(n):
+            if e == r or not kept[r][e]:
+                continue
+            rs = runs_of(kept[r][e])
+            parts = 1 if len(rs) <= BIG else -(-len(rs) // PIECE)
+            o = off[r][e]
+            for i in range(parts):
+                part = rs[i * len(rs) // parts:(i + 1) * len(rs) // parts]
+                w = sum(q[1] for q in part)
+                pieces.append((r, e, o, part, w))
+                o += w
+
+    def uses(i, s):
+        r, e, o, part, w = pieces[i]
+        a, b, d = s // 8, cores[e] // 8, topo.die(s)
+        out = [(("core", s), len(part) + 1)]
+        if a != b:
+            if topo.same_plane(a, b):
+                out += [(("out", a, d), w), (("in", b, d), w)]
+            else:
+                out += [(("mate", a, d), w)]
+                if not topo.mates(a, b):
+                    out += [(("out", a ^ 1, d), w), (("in", b, d), w)]
+        return out
+
+    load, share = {}, {}
+    opts = []
+    for i in range(len(pieces)):
+        r, e = pieces[i][0], pieces[i][1]
+        opts.append([s for s in team[r] if topo.may_write(s, cores[e])])
+        for key, v in uses(i, opts[i][0]):
+            k = ("core", r) if key[0] == "core" else key[:2]
+            share[k] = share.get(k, 0) + v
+    for r in range(n):
+        base = 5 + len(runs_of(kept[r][r]))
+        load[("core", cores[r])] = base
+        share[("core", r)] = share.get(("core", r), 0) + base
+
+    def fair(key):
+        return share[("core", leader[key[1]])] / 4.0 if key[0] == "core" else share[key[:2]] / 2.0
+
+    def rise(us):
+        return sum(((load.get(k, 0) + v) / fair(k)) ** POWER - (load.get(k, 0) / fair(k)) ** POWER for k, v in us)
+
+    def book(us, sign):
+        for k, v in us:
+            load[k] = load.get(k, 0) + sign * v
+
+    order = sorted(range(len(pieces)), key=lambda i: (-len(pieces[i][3]), i))
+    who = {}
+    for i in order:
+        who[i] = min(opts[i], key=lambda s: (rise(uses(i, s)), s))
+        book(uses(i, who[i]), 1)
+    for sweep in range(3):
+        for i in order:
+            book(uses(i, who[i]), -1)
+            who[i] = min(opts[i], key=lambda s: (rise(uses(i, s)), s != who[i], s))
+            book(uses(i, who[i]), 1)
+
+    msgs = {}
+    for i in range(len(pieces)):
+        r, e, o, part, w = pieces[i]
+        m = msgs.setdefault(who[i], [])
+        if m and m[-1][0] == e and m[-1][1] + m[-1][3] == o:
+            m[-1] = (e, m[-1][1], runs_of([t + j for t, l in m[-1][2] + part for j in range(l)]), m[-1][3] + w)
         else:
-            out.append([t, 1])
-    return out
-
-
-def relay_of(core):
-    return (core // 8) * 8 + 6
-
-
-def bits(m):
-    return bin(m).count("1")
-
-
-def layout(r, T, topo, n, kept):
-    c = T.cores[r]
-    direct = [e for e in range(n) if e != r and kept[r][e] and topo.may_write(c, T.cores[e])]
-    relay = [e for e in range(n) if e != r and kept[r][e] and not topo.may_write(c, T.cores[e])]
-    pos = {}
-    o = 0
-    for e in direct + relay:
-        pos[e] = o
-        o += len(kept[r][e])
-    return direct, relay, pos, o
+            m.append((e, o, part, w))
+    arrive = [0] * n
+    for s in msgs:
+        msgs[s].sort(key=lambda q: ((cores[q[0]] // 8 - s // 8) % 16, q[0], q[1]))
+        for q in msgs[s]:
+            arrive[q[0]] += bin(topo.mask(s, cores[q[0]])).count("1")
+    CACHE["plan"] = (kept, off, cnt, msgs, arrive, leader)
+    return CACHE["plan"]
 
 
 def rank_program(g, core, T, topo):
-    n, kept, off, cnt = make_plan(T)
-    rank = T.rank_of(core)
-    S = T.sem
-
-    def send(src_ap, e, r):
-        dst = T.cores[e]
-        rid, pid, _se = topo.addr(dst)
-        m = topo.mask(core, dst)
-        w = len(kept[r][e])
-        g.remote_dma(T.land[:, off[r][e]:off[r][e] + w], src_ap, S.arrived, S.sent, pid, rid, m)
-        return bits(m)
-
-    if rank is None:
-        if core % 8 != 6:
-            return
-        src = (core // 8) * 8 + 1
-        r = T.rank_of(src)
-        if r is None:
-            return
-        direct, relay, pos, tot = layout(r, T, topo, n, kept)
-        if not relay:
-            return
-        g.wait_ge(S.relin, 16)
-        base = pos[relay[0]]
-        s = 0
-        for e in relay:
-            w = len(kept[r][e])
-            s += send(T.rel[:, pos[e] - base:pos[e] - base + w], e, r)
-        g.wait_ge(S.sent, s)
+    kept, off, cnt, msgs, arrive, leader = make_plan(T, topo)
+    if core not in leader:
         return
+    S = T.sem
+    rank = T.rank_of(core)
+    r = leader[core]
+    mine = msgs.get(core, [])
+    queues = [g.sync, g.scalar]
+    sent = 0
 
-    r = rank
-    direct, relay, pos, tot = layout(r, T, topo, n, kept)
-    g.sync.dma_start(T.xs[:], T.x[:]).then_inc(S.loaded, 16)
-    g.sync.wait_ge(S.loaded, 16)
-    g.scalar.wait_ge(S.loaded, 16)
-    qs = [g.sync, g.scalar]
-    k = 0
-    for e in direct + relay + [r]:
-        o = off[r][r] if e == r else pos[e]
-        buf = T.land if e == r else T.pk
-        for t, w in runs_of(kept[r][e]):
-            qs[k % 2].dma_start(buf[:, o:o + w], T.xs[:, t:t + w]).then_inc(S.packed, 16)
-            o += w
+    if rank is not None:
+        g.sync.dma_start(T.xs[:], T.x[:]).then_inc(S.loaded, 16)
+        for q in (g, g.sync, g.scalar):
+            q.wait_ge(S.loaded, 16)
+        helpers = [s for s in sorted(leader) if leader[s] == r and s != core]
+        ids = [DstId(rid=topo.addr(s)[0], pnc=topo.addr(s)[1]) for s in helpers]
+        g.remote_dma_fused([RemoteDMATransfer(dst_ids=ids, dma_engine_mask=0xFFFF, remote_sem=S.xin,
+                                              srcs=[T.xs[:]], dsts=[T.xs[:] for s in helpers], alu_op=0)],
+                           local_sem=S.sent)
+        sent += 16
+    else:
+        for q in (g, g.sync, g.scalar):
+            q.wait_ge(S.xin, 16)
+
+    turn = [0]
+
+    def gather(buf, o, runs, sem):
+        k = 0
+        for t, step, m in segments(runs):
+            src = T.xs[:, t:t + (m - 1) * step + 1:step, :]
+            queues[turn[0] % 2].dma_start(buf[:, o:o + m, :], src).then_inc(sem, 16)
+            turn[0] += 1
+            o += m
             k += 1
-    g.wait_ge(S.packed, 16 * k)
-    s = 0
-    if relay:
-        base = pos[relay[0]]
-        rc = relay_of(core)
-        rid, pid, _se = topo.addr(rc)
-        g.remote_dma(T.rel[:, 0:tot - base], T.pk[:, base:tot], S.relin, S.sent, pid, rid, 0xFFFF)
-        s += 16
-    for e in direct:
-        w = len(kept[r][e])
-        s += send(T.pk[:, pos[e]:pos[e] + w], e, r)
-    a = 0
-    for q in range(n):
-        if q != r and kept[q][r]:
-            sc = T.cores[q]
-            if not topo.may_write(sc, core):
-                sc = relay_of(sc)
-            a += bits(topo.mask(sc, core))
-    g.sync.wait_ge(S.packed, 16 * k)
-    g.sync.wait_ge(S.arrived, a)
-    g.sync.dma_start(T.y[:, 0:cnt[r]], T.land[:, 0:cnt[r]]).then_inc(S.stored, 16)
-    g.sync.wait_ge(S.stored, 16)
-    g.wait_ge(S.sent, s)
-    g.wait_ge(S.arrived, a)
-    g.wait_ge(S.stored, 16)
+        return k
+
+    per = -(-len(mine) // NPK) if mine else 1
+    need = [0] * NPK
+    pos = []
+    o = 0
+    for j in range(len(mine)):
+        e, col, runs, w = mine[j]
+        need[j // per] += 16 * gather(T.pk, o, runs, S["pk%d" % (j // per)])
+        pos.append(o)
+        o += w
+    own = 0
+    if rank is not None and kept[r][r]:
+        own = 16 * gather(T.land, off[r][r], runs_of(kept[r][r]), S.own)
+
+    for j in range(len(mine)):
+        e, col, runs, w = mine[j]
+        if j % per == 0:
+            g.wait_ge(S["pk%d" % (j // per)], need[j // per])
+        dst = T.cores[e]
+        rid, pid, ring = topo.addr(dst)
+        m = topo.mask(core, dst)
+        g.remote_dma(T.land[:, col:col + w, :], T.pk[:, pos[j]:pos[j] + w, :], S.arrived, S.sent, pid, rid, m)
+        sent += bin(m).count("1")
+
+    if rank is not None:
+        if own:
+            g.sync.wait_ge(S.own, own)
+        g.sync.wait_ge(S.arrived, arrive[r])
+        g.sync.dma_start(T.y[:, 0:cnt[r]], T.land[:, 0:cnt[r], :]).then_inc(S.stored, 16)
+        g.wait_ge(S.stored, 16)
+    g.wait_ge(S.sent, sent)

@@ -1,12 +1,11 @@
 from concourse.bass import DstId, RemoteDMATransfer
 
-STEPPED = False
 NPK = 16
 
 SCRATCH = {
-    "xs": ("sbuf", [128, 512, 1], "float32"),
-    "pk": ("sbuf", [128, 512, 1], "float32"),
-    "land": ("sbuf", [128, 387, 1], "float32"),
+    "xs": ("sbuf", [128, 512], "float32"),
+    "pk": ("sbuf", [128, 512], "float32"),
+    "land": ("sbuf", [128, 387], "float32"),
 }
 SEMAPHORES = ["loaded", "xin", "own", "sent", "arrived", "stored"] + ["pk%d" % i for i in range(NPK)]
 
@@ -23,40 +22,6 @@ def runs_of(tokens):
             out[-1][1] += 1
         else:
             out.append([t, 1])
-    return out
-
-
-def segments(runs):
-    out = []
-    i = 0
-    while i < len(runs):
-        if runs[i][1] > 1 or not STEPPED:
-            out.append((runs[i][0], 1, runs[i][1]))
-            i += 1
-            continue
-        j = i
-        while j < len(runs) and runs[j][1] == 1:
-            j += 1
-        ts = [q[0] for q in runs[i:j]]
-        m = len(ts)
-        best = [0] + [m + 1] * m
-        prev = [0] * (m + 1)
-        for a in range(m):
-            b = a + 1
-            while True:
-                if best[a] + 1 < best[b]:
-                    best[b] = best[a] + 1
-                    prev[b] = a
-                if b >= m or (b - a >= 2 and ts[b] - ts[b - 1] != ts[a + 1] - ts[a]):
-                    break
-                b += 1
-        cuts = [m]
-        while cuts[-1] > 0:
-            cuts.append(prev[cuts[-1]])
-        cuts.reverse()
-        for a, b in zip(cuts[:-1], cuts[1:]):
-            out.append((ts[a], ts[a + 1] - ts[a] if b - a > 1 else 1, b - a))
-        i = j
     return out
 
 
@@ -190,14 +155,11 @@ def rank_program(g, core, T, topo):
     turn = [0]
 
     def gather(buf, o, runs, sem):
-        k = 0
-        for t, step, m in segments(runs):
-            src = T.xs[:, t:t + (m - 1) * step + 1:step, :]
-            queues[turn[0] % 2].dma_start(buf[:, o:o + m, :], src).then_inc(sem, 16)
+        for t, w in runs:
+            queues[turn[0] % 2].dma_start(buf[:, o:o + w], T.xs[:, t:t + w]).then_inc(sem, 16)
             turn[0] += 1
-            o += m
-            k += 1
-        return k
+            o += w
+        return 16 * len(runs)
 
     per = -(-len(mine) // NPK) if mine else 1
     need = [0] * NPK
@@ -205,12 +167,12 @@ def rank_program(g, core, T, topo):
     o = 0
     for j in range(len(mine)):
         e, col, runs, w = mine[j]
-        need[j // per] += 16 * gather(T.pk, o, runs, S["pk%d" % (j // per)])
+        need[j // per] += gather(T.pk, o, runs, S["pk%d" % (j // per)])
         pos.append(o)
         o += w
     own = 0
     if rank is not None and kept[r][r]:
-        own = 16 * gather(T.land, off[r][r], runs_of(kept[r][r]), S.own)
+        own = gather(T.land, off[r][r], runs_of(kept[r][r]), S.own)
 
     for j in range(len(mine)):
         e, col, runs, w = mine[j]
@@ -219,13 +181,13 @@ def rank_program(g, core, T, topo):
         dst = T.cores[e]
         rid, pid, ring = topo.addr(dst)
         m = topo.mask(core, dst)
-        g.remote_dma(T.land[:, col:col + w, :], T.pk[:, pos[j]:pos[j] + w, :], S.arrived, S.sent, pid, rid, m)
+        g.remote_dma(T.land[:, col:col + w], T.pk[:, pos[j]:pos[j] + w], S.arrived, S.sent, pid, rid, m)
         sent += bin(m).count("1")
 
     if rank is not None:
         if own:
             g.sync.wait_ge(S.own, own)
         g.sync.wait_ge(S.arrived, arrive[r])
-        g.sync.dma_start(T.y[:, 0:cnt[r]], T.land[:, 0:cnt[r], :]).then_inc(S.stored, 16)
+        g.sync.dma_start(T.y[:, 0:cnt[r]], T.land[:, 0:cnt[r]]).then_inc(S.stored, 16)
         g.wait_ge(S.stored, 16)
     g.wait_ge(S.sent, sent)

from concourse.bass import DstId, RemoteDMATransfer

NPK = 16

SCRATCH = {
    "xs": ("sbuf", [128, 512], "float32"),
    "pk": ("sbuf", [128, 512], "float32"),
    "land": ("sbuf", [128, 387], "float32"),
}
SEMAPHORES = ["loaded", "xin", "own", "sent", "arrived", "stored"] + ["pk%d" % i for i in range(NPK)]

TEAM = {1: (1, 3, 5, 7), 2: (2, 0, 4, 6)}
BIG, PIECE = 24, 10
POWER = 8
CACHE = {}


def runs_of(tokens):
    out = []
    for t in tokens:
        if out and out[-1][0] + out[-1][1] == t:
            out[-1][1] += 1
        else:
            out.append([t, 1])
    return out


def make_plan(T, topo):
    if "plan" in CACHE:
        return CACHE["plan"]
    route, cap, cores = T.tables["ROUTE"], T.tables["CAP"], T.cores
    n = len(route)
    fill = [0] * n
    kept = [[[] for _ in range(n)] for _ in range(n)]
    off = [[0] * n for _ in range(n)]
    for r in range(n):
        for t in range(len(route[r])):
            for e in route[r][t]:
                if fill[e] < cap:
                    if not kept[r][e]:
                        off[r][e] = fill[e]
                    kept[r][e].append(t)
                fill[e] += 1
    cnt = [min(f, cap) for f in fill]

    team = [[cores[r] // 8 * 8 + k for k in TEAM[cores[r] % 8]] for r in range(n)]
    leader = {}
    for r in range(n):
        for s in team[r]:
            leader[s] = r

    pieces = []
    for r in range(n):
        for e in range(n):
            if e == r or not kept[r][e]:
                continue
            rs = runs_of(kept[r][e])
            parts = 1 if len(rs) <= BIG else -(-len(rs) // PIECE)
            o = off[r][e]
            for i in range(parts):
                part = rs[i * len(rs) // parts:(i + 1) * len(rs) // parts]
                w = sum(q[1] for q in part)
                pieces.append((r, e, o, part, w))
                o += w

    def uses(i, s):
        r, e, o, part, w = pieces[i]
        a, b, d = s // 8, cores[e] // 8, topo.die(s)
        out = [(("core", s), len(part) + 1)]
        if a != b:
            if topo.same_plane(a, b):
                out += [(("out", a, d), w), (("in", b, d), w)]
            else:
                out += [(("mate", a, d), w)]
                if not topo.mates(a, b):
                    out += [(("out", a ^ 1, d), w), (("in", b, d), w)]
        return out

    load, share = {}, {}
    opts = []
    for i in range(len(pieces)):
        r, e = pieces[i][0], pieces[i][1]
        opts.append([s for s in team[r] if topo.may_write(s, cores[e])])
        for key, v in uses(i, opts[i][0]):
            k = ("core", r) if key[0] == "core" else key[:2]
            share[k] = share.get(k, 0) + v
    for r in range(n):
        base = 5 + len(runs_of(kept[r][r]))
        load[("core", cores[r])] = base
        share[("core", r)] = share.get(("core", r), 0) + base

    def fair(key):
        return share[("core", leader[key[1]])] / 4.0 if key[0] == "core" else share[key[:2]] / 2.0

    def rise(us):
        return sum(((load.get(k, 0) + v) / fair(k)) ** POWER - (load.get(k, 0) / fair(k)) ** POWER for k, v in us)

    def book(us, sign):
        for k, v in us:
            load[k] = load.get(k, 0) + sign * v

    order = sorted(range(len(pieces)), key=lambda i: (-len(pieces[i][3]), i))
    who = {}
    for i in order:
        who[i] = min(opts[i], key=lambda s: (rise(uses(i, s)), s))
        book(uses(i, who[i]), 1)
    for sweep in range(3):
        for i in order:
            book(uses(i, who[i]), -1)
            who[i] = min(opts[i], key=lambda s: (rise(uses(i, s)), s != who[i], s))
            book(uses(i, who[i]), 1)

    msgs = {}
    for i in range(len(pieces)):
        r, e, o, part, w = pieces[i]
        m = msgs.setdefault(who[i], [])
        if m and m[-1][0] == e and m[-1][1] + m[-1][3] == o:
            m[-1] = (e, m[-1][1], runs_of([t + j for t, l in m[-1][2] + part for j in range(l)]), m[-1][3] + w)
        else:
            m.append((e, o, part, w))
    arrive = [0] * n
    for s in msgs:
        msgs[s].sort(key=lambda q: ((cores[q[0]] // 8 - s // 8) % 16, q[0], q[1]))
        for q in msgs[s]:
            arrive[q[0]] += bin(topo.mask(s, cores[q[0]])).count("1")
    CACHE["plan"] = (kept, off, cnt, msgs, arrive, leader)
    return CACHE["plan"]


def rank_program(g, core, T, topo):
    kept, off, cnt, msgs, arrive, leader = make_plan(T, topo)
    if core not in leader:
        return
    S = T.sem
    rank = T.rank_of(core)
    r = leader[core]
    mine = msgs.get(core, [])
    queues = [g.sync, g.scalar]
    sent = 0

    if rank is not None:
        g.sync.dma_start(T.xs[:], T.x[:]).then_inc(S.loaded, 16)
        for q in (g, g.sync, g.scalar):
            q.wait_ge(S.loaded, 16)
        helpers = [s for s in sorted(leader) if leader[s] == r and s != core]
        ids = [DstId(rid=topo.addr(s)[0], pnc=topo.addr(s)[1]) for s in helpers]
        g.remote_dma_fused([RemoteDMATransfer(dst_ids=ids, dma_engine_mask=0xFFFF, remote_sem=S.xin,
                                              srcs=[T.xs[:]], dsts=[T.xs[:] for s in helpers], alu_op=0)],
                           local_sem=S.sent)
        sent += 16
    else:
        for q in (g, g.sync, g.scalar):
            q.wait_ge(S.xin, 16)

    turn = [0]

    def gather(buf, o, runs, sem):
        for t, w in runs:
            queues[turn[0] % 2].dma_start(buf[:, o:o + w], T.xs[:, t:t + w]).then_inc(sem, 16)
            turn[0] += 1
            o += w
        return 16 * len(runs)

    per = -(-len(mine) // NPK) if mine else 1
    need = [0] * NPK
    pos = []
    o = 0
    for j in range(len(mine)):
        e, col, runs, w = mine[j]
        need[j // per] += gather(T.pk, o, runs, S["pk%d" % (j // per)])
        pos.append(o)
        o += w
    own = 0
    if rank is not None and kept[r][r]:
        own = gather(T.land, off[r][r], runs_of(kept[r][r]), S.own)

    for j in range(len(mine)):
        e, col, runs, w = mine[j]
        if j % per == 0:
            g.wait_ge(S["pk%d" % (j // per)], need[j // per])
        dst = T.cores[e]
        rid, pid, ring = topo.addr(dst)
        m = topo.mask(core, dst)
        g.remote_dma(T.land[:, col:col + w], T.pk[:, pos[j]:pos[j] + w], S.arrived, S.sent, pid, rid, m)
        sent += bin(m).count("1")

    if rank is not None:
        if own:
            g.sync.wait_ge(S.own, own)
        g.sync.wait_ge(S.arrived, arrive[r])
        g.sync.dma_start(T.y[:, 0:cnt[r]], T.land[:, 0:cnt[r]]).then_inc(S.stored, 16)
        g.wait_ge(S.stored, 16)
    g.wait_ge(S.sent, sent)
